import numpy as np
import ml_dtypes


def mxq(x, axis, fmt="e4m3"):
    dtype, down = {"e4m3": (ml_dtypes.float8_e4m3fn, 7), "e5m2": (ml_dtypes.float8_e5m2, 14)}[fmt]
    v = np.moveaxis(np.asarray(x, np.float32).astype(ml_dtypes.bfloat16).astype(np.float64), axis, -1)
    blocks = v.reshape(v.shape[:-1] + (-1, 32))
    amax = np.abs(blocks).max(-1, keepdims=True)
    byte = np.maximum(np.where(amax > 0, np.frexp(amax)[1] - 1 + 127, 0) - down, 1)
    scale = np.exp2(byte - 127.0)
    codes = (blocks / scale).astype(np.float32).astype(dtype).astype(np.float64)
    return np.moveaxis((codes * scale).reshape(v.shape), -1, axis)


WIDE = False


def mx_kscale(k):
    if not WIDE:
        return np.ones(k)
    levels = np.array([10, -10, 5, -5, 0])
    if k % 512:
        return np.exp2(np.random.permutation(np.resize(levels, k // 32))).repeat(32)
    a = np.empty((k // 512, 16))
    for p in range(k // 512):
        a[p, :8] = np.random.permutation(np.resize(levels, 8))
        for g in range(8):
            far = levels[np.abs(levels - a[p, g]) >= 10]
            a[p, g + 8] = far[np.random.randint(len(far))]
    return np.exp2(a.ravel()).repeat(32)


def f64(x):
    return np.asarray(x).astype(np.float64)


def striped(idx):
    return np.tile(idx.reshape(-1, 16).T, (8, 1)).astype(np.uint16)


def unstriped(offs):
    return offs[:16].T.reshape(-1).astype(np.int64)


E2M1 = np.array([0.0, 0.5, 1.0, 1.5, 2.0, 3.0, 4.0, 6.0, -0.0, -0.5, -1.0, -1.5, -2.0, -3.0, -4.0, -6.0])


def pack_weight(w, fmt):
    k, n = w.shape
    w = f64(np.asarray(w, np.float32).astype(ml_dtypes.bfloat16)).reshape(k // 32, 32, n)
    amax = np.abs(w).max(1)
    if fmt == "e4m3":
        byte = np.frexp(amax)[1] - 1 + 127 - 7
    else:
        mant, ex = np.frexp(amax / 6.0)
        byte = np.where(mant > 0.5, ex, ex - 1) + 127
    byte = np.clip(np.where(amax > 0, byte, 1), 1, 254)
    scaled = (w * np.exp2(127.0 - byte)[:, None, :]).reshape(k, n).astype(np.float32)
    by_word = np.ascontiguousarray(scaled.reshape(k // 512, 128, 4, n).transpose(0, 1, 3, 2))
    if fmt == "e4m3":
        words = by_word.astype(ml_dtypes.float8_e4m3fn).view(np.uint8)
    else:
        c = by_word.astype(ml_dtypes.float4_e2m1fn).view(np.uint8) & 0xF
        words = (c[..., 0::2] | (c[..., 1::2] << 4)).reshape(k // 512, 128, 2 * n)
    return np.ascontiguousarray(words), np.ascontiguousarray(byte.astype(np.uint8).reshape(k // 512, 16, n))


def unpack_weight(words, scales, fmt):
    g, _, n = scales.shape
    words = np.ascontiguousarray(words).reshape(g, 128, n, -1)
    if fmt == "e4m3":
        vals = words.view(ml_dtypes.float8_e4m3fn).astype(np.float64)
    else:
        nib = np.empty((g, 128, n, 4), np.uint8)
        nib[..., 0::2] = words & 0xF
        nib[..., 1::2] = words >> 4
        vals = E2M1[nib]
    vals = vals * np.repeat(np.exp2(scales.astype(np.float64) - 127.0), 8, axis=1)[..., None]
    return vals.transpose(0, 1, 3, 2).reshape(g * 512, n)


def silu(v):
    return v / (1.0 + np.exp(-np.maximum(v, -700.0)))


K, T, E, H, N = 1024, 512, 2, 512, 384
COUNTS = (128, 384)
STARTS = np.cumsum((0,) + COUNTS)


def by_expert(wq, xq):
    return np.concatenate([wq[e].T @ xq[:, STARTS[e]:STARTS[e + 1]] for e in range(E)], axis=1)


def setup_inputs():
    n = np.random.standard_normal
    s = mx_kscale(K)[:, None]
    u = mx_kscale(H)
    expert = np.random.permutation(np.repeat(np.arange(E), COUNTS))
    slot_token = np.argsort(expert, kind="stable")
    w1 = [pack_weight(m, "e2m1") for m in n((E, K, H)) / np.sqrt(K) / s[None]]
    w3 = [pack_weight(m, "e2m1") for m in n((E, K, H)) / np.sqrt(K) / s[None] * u[None, None, :]]
    w2 = [pack_weight(m, "e2m1") for m in n((E, H, N)) / np.sqrt(H) / u[None, :, None]]
    return {
        "xT": (n((K, T)) * s).astype(np.float32),
        "w1_words": np.stack([m[0] for m in w1]),
        "w1_scales": np.stack([m[1] for m in w1]),
        "w3_words": np.stack([m[0] for m in w3]),
        "w3_scales": np.stack([m[1] for m in w3]),
        "w2_words": np.stack([m[0] for m in w2]),
        "w2_scales": np.stack([m[1] for m in w2]),
        "gate": np.tile(np.random.uniform(0.2, 1.0, T), (N, 1)).astype(np.float32),
        "offs": striped(slot_token),
    }


def reference(xT, w1_words, w1_scales, w3_words, w3_scales, w2_words, w2_scales, gate, offs):
    idx = unstriped(offs)
    w1 = np.stack([unpack_weight(w1_words[e], w1_scales[e], "e2m1") for e in range(E)])
    w3 = np.stack([unpack_weight(w3_words[e], w3_scales[e], "e2m1") for e in range(E)])
    w2 = np.stack([unpack_weight(w2_words[e], w2_scales[e], "e2m1") for e in range(E)])
    xq = mxq(f64(xT)[:, idx], 0, "e4m3")
    h = silu(by_expert(w1, xq))
    h = h * by_expert(w3, xq)
    y = by_expert(w2, mxq(h, 0, "e4m3"))
    out = np.zeros((N, T))
    out[:, idx] = f64(gate) * y
    return out

@@ -1,0 +1,299 @@
+from contextlib import ExitStack
+
+import concourse.mybir as mybir
+from concourse.masks import make_identity
+
+K, T, E, H, N = 1024, 512, 2, 512, 384
+
+F32 = mybir.dt.float32
+BF16 = mybir.dt.bfloat16
+I32 = mybir.dt.int32
+U32 = mybir.dt.uint32
+U16 = mybir.dt.uint16
+U8 = mybir.dt.uint8
+FP8X4 = mybir.dt.float8_e4m3fn_x4
+FP4X4 = mybir.dt.float4_e2m1fn_x4
+ACT = mybir.ActivationFunctionType
+MULT = mybir.AluOpType.mult
+
+P = 128
+PASSES = K // 512
+HALF = T // 2
+VECTOR_COLUMNS = ((192, 192), (0, 160))
+TILES = T // P
+N_TILES = N // P
+GROUPS = ((0, 128), (128, 384), (384, 512))
+
+FLOPS = 2 * T * (2 * K * H + H * N)
+BYTES = 4 * K * T + 2 * E * (K * H // 2 + K * H // 32) + E * (H * N // 2 + H * N // 32) + 4 * P * T + 2 * P * (T // 16) + 4 * N * T
+
+
+def tile_moe_rag_glu_silu_kernel(
+    tc, xT, w1_words, w1_scales, w3_words, w3_scales, w2_words, w2_scales, gate, offs, out
+):
+    nc = tc.nc
+    with ExitStack() as ctx:
+        keep = ctx.enter_context(tc.tile_pool(name="keep", bufs=1))
+        work = ctx.enter_context(tc.tile_pool(name="work", bufs=3))
+        psum_ab = ctx.enter_context(tc.psum_pool(name="psum_ab", bufs=3))
+        psum_one = ctx.enter_context(tc.psum_pool(name="psum_one", bufs=1))
+
+        offsets = keep.tile([P, T // 16], U16, name="offsets")
+
+        def scale_plane(name, scales):
+            plane = keep.tile([P, E * scales.shape[1], scales.shape[3]], U8, name=f"{name}_plane", align_bytes=64)
+            nc.vector.memset(plane[:].bitcast(I32), 0)
+            return plane
+
+        def load_scales(queue, plane, scales):
+            rows = scales.bitcast(I32).rearrange("e s q i -> q (e s) i")
+            for q in range(4):
+                queue.dma_start(plane[32 * q : 32 * q + 4, :, :].bitcast(I32), rows[4 * q : 4 * q + 4, :, :])
+
+        def load_x(s):
+            rows = xT[s * 512 : (s + 1) * 512, :].rearrange("(p j) w -> p j w", j=4)
+            halves = []
+            for half in range(2):
+                raw = keep.tile([P, 4, HALF], F32, name=f"x_raw_{s}_{half}")
+                nc.sync.dma_start(raw[:], rows[:, :, half * HALF : (half + 1) * HALF])
+                halves.append(raw)
+            return halves
+
+        def load_words(name, words, e):
+            codes = keep.tile([P, words.shape[1], words.shape[3]], U8, name=f"{name}_codes_{e}", align_bytes=64)
+            nc.sync.dma_start(codes[:].bitcast(I32), words.bitcast(I32)[e].rearrange("s p b -> p s b"))
+            return codes
+
+        w1_sc = scale_plane("w1", w1_scales)
+        w3_sc = scale_plane("w3", w3_scales)
+        w2_sc = scale_plane("w2", w2_scales)
+        all_bytes = []
+        for s in range(PASSES):
+            plane = keep.tile([P, T], U8, name=f"all_bytes_{s}", align_bytes=64)
+            nc.vector.memset(plane[:].bitcast(I32), 0)
+            all_bytes.append(plane)
+
+        x_raw = [load_x(0)]
+        nc.sync.dma_start(offsets[:], offs)
+        load_scales(nc.sync, w1_sc, w1_scales)
+        x_raw.append(load_x(1))
+        load_scales(nc.sync, w3_sc, w3_scales)
+        w1, w3 = [], []
+        for e in range(E):
+            w1.append(load_words("w1", w1_words, e))
+            w3.append(load_words("w3", w3_words, e))
+        load_scales(nc.sync, w2_sc, w2_scales)
+        w2 = keep.tile([P, E, 2 * N], U8, name="w2", align_bytes=64)
+        nc.sync.dma_start(w2[:].bitcast(I32), w2_words.bitcast(I32)[:, 0].rearrange("e p b -> p e b"))
+
+        gate_sb = keep.tile([P, T], F32, name="gate_sb")
+        nc.sync.dma_start(gate_sb[:], gate[0:P, :])
+
+        ident = keep.tile([P, P], F32, name="ident")
+        make_identity(nc, ident[:])
+
+        warm = keep.tile([P, 1], F32, name="warm")
+        nc.vector.memset(warm[:], 0.0)
+        warm_out = keep.tile([P, 1], F32, name="warm_out")
+        nc.scalar.activation(warm_out[:], warm[:], ACT.Silu)
+
+        grouped, all_words, x_words, x_bytes = {}, [], [], []
+        for s in range(PASSES):
+            words = keep.tile([P, T], U32, name=f"all_words_{s}", align_bytes=64)
+            slot_words = keep.tile([P, T], U32, name=f"slot_words_{s}", align_bytes=64)
+            slot_bytes = keep.tile([P, T], U8, name=f"slot_bytes_{s}", align_bytes=64)
+            all_words.append(words)
+            x_words.append(slot_words)
+            x_bytes.append(slot_bytes)
+            for half in range(2):
+                tokens = keep.tile([P, HALF, 4], BF16, name=f"grouped_{s}_{half}", align_bytes=64)
+                grouped[s, half] = tokens
+        out_sb = []
+        for n in range(N_TILES):
+            window = keep.tile([P, T], F32, name=f"out_sb_{n}")
+            out_sb.append(window)
+        sums, acts, hidden, turned, h_grouped, h_codes, y_sums, y_sb = {}, {}, {}, {}, {}, {}, {}, {}
+
+        def cast(engine_copy, s, half, lo, hi):
+            engine_copy(
+                grouped[s, half][:, lo:hi, :].rearrange("p (c i) j -> p c j i", i=4),
+                x_raw[s][half][:, :, lo:hi].rearrange("p j (c i) -> p c j i", i=4),
+            )
+
+        def cast_s(s, half):
+            cast(nc.scalar.copy, s, half, VECTOR_COLUMNS[s][half], HALF)
+
+        def cast_v(s, half):
+            cast(nc.vector.tensor_copy, s, half, 0, VECTOR_COLUMNS[s][half])
+
+        def quantise_x(s, half):
+            cols = slice(half * HALF, (half + 1) * HALF)
+            nc.vector.quantize_mx(
+                out=all_words[s][:, cols].bitcast(FP8X4),
+                scales=all_bytes[s][:, cols],
+                in_=grouped[s, half][:].rearrange("p w j -> p (w j)"),
+            )
+
+        def gather(picked, tokens, group):
+            lo, hi = GROUPS[group]
+            nc.vector.tensor_copy(picked[:, lo:hi], tokens[:].indirect(offsets[:, lo // 16 : hi // 16]))
+
+        def gather_words(s, group):
+            gather(x_words[s], all_words[s], group)
+
+        def gather_bytes(s, group):
+            gather(x_bytes[s], all_bytes[s], group)
+
+        def first_layer(t, s):
+            e = 0 if t == 0 else 1
+            cols = slice(t * P, (t + 1) * P)
+            if s == 0:
+                a = psum_ab.tile([P, H], F32, name="a")
+                b = psum_ab.tile([P, H], F32, name="b")
+                sums[t] = (a, b)
+            for acc, codes, plane in zip(sums[t], (w1, w3), (w1_sc, w3_sc)):
+                nc.tensor.matmul_mx(
+                    out=acc[:],
+                    lhsT=x_words[s][:, cols].bitcast(FP8X4),
+                    lhsT_scale=x_bytes[s][:, cols],
+                    rhs=codes[e][:, s, :].bitcast(FP4X4),
+                    rhs_scale=plane[:, PASSES * e + s, :],
+                    start=(s == 0),
+                    stop=(s == PASSES - 1),
+                )
+
+        def silu(t):
+            act = work.tile([P, H], F32, name="act")
+            nc.scalar.activation(act[:], sums[t][0][:], ACT.Silu)
+            acts[t] = act
+
+        def multiply(t):
+            h = work.tile([P, 2, P, 2], BF16, name="h", align_bytes=64)
+            nc.vector.tensor_tensor(
+                h[:],
+                acts[t][:].rearrange("p (q u d) -> p u q d", u=2, d=2),
+                sums[t][1][:].rearrange("p (q u d) -> p u q d", u=2, d=2),
+                MULT,
+            )
+            hidden[t] = h
+
+        def turn(t):
+            bank = psum_one.tile([P, 2, P], F32, name="turned")
+            pairs = hidden[t][:].rearrange("p u q d -> p (u q d)").bitcast(F32)
+            for u in range(2):
+                nc.tensor.transpose(bank[:, u, :], pairs[:, u * P : (u + 1) * P], ident[:])
+            turned[t] = bank
+
+        def group_h(t):
+            h4 = work.tile([P, P, 4], BF16, name="h4", align_bytes=64)
+            nc.scalar.copy(h4[:].bitcast(F32), turned[t][:].rearrange("p u r -> p r u"))
+            h_grouped[t] = h4
+
+        def quantise_h(t):
+            h_words = work.tile([P, P], U32, name="h_words", align_bytes=64)
+            h_bytes = work.tile([P, P], U8, name="h_bytes", align_bytes=64)
+            nc.vector.quantize_mx(
+                out=h_words[:].bitcast(FP8X4), scales=h_bytes[:], in_=h_grouped[t][:].rearrange("p r j -> p (r j)")
+            )
+            h_codes[t] = (h_words, h_bytes)
+
+        def second_layer(t):
+            e = 0 if t == 0 else 1
+            h_words, h_bytes = h_codes[t]
+            y = psum_one.tile([P, N_TILES, P], F32, name="y")
+            for n in range(N_TILES):
+                nc.tensor.matmul_mx(
+                    out=y[:, n, :],
+                    lhsT=w2[:, e, 2 * P * n : 2 * P * (n + 1)].bitcast(FP4X4),
+                    lhsT_scale=w2_sc[:, e, P * n : P * (n + 1)],
+                    rhs=h_words[:].bitcast(FP8X4),
+                    rhs_scale=h_bytes[:],
+                    start=True,
+                    stop=True,
+                )
+            y_sums[t] = y
+
+        def empty_y(t):
+            result = work.tile([P, N_TILES, P], F32, name="result")
+            nc.scalar.copy(result[:], y_sums[t][:])
+            y_sb[t] = result
+
+        def scatter(t, n):
+            cols = slice(t * P, (t + 1) * P)
+            where = offsets[:, t * P // 16 : (t + 1) * P // 16]
+            nc.vector.tensor_tensor(out_sb[n][:].indirect(where), y_sb[t][:, n, :], gate_sb[:, cols], MULT)
+
+        cast_s(0, 0)
+        cast_v(0, 0)
+        quantise_x(0, 0)
+        cast_s(0, 1)
+        cast_v(0, 1)
+        cast_s(1, 0)
+        quantise_x(0, 1)
+        gather_words(0, 0)
+        gather_words(0, 1)
+        cast_s(1, 1)
+        gather_bytes(0, 0)
+        cast_v(1, 1)
+        quantise_x(1, 0)
+        quantise_x(1, 1)
+        gather_bytes(0, 1)
+        gather_words(1, 0)
+        gather_bytes(1, 0)
+        first_layer(0, 0)
+        gather_bytes(1, 1)
+        first_layer(0, 1)
+        silu(0)
+        first_layer(1, 0)
+        gather_words(1, 1)
+        first_layer(1, 1)
+        silu(1)
+        first_layer(2, 0)
+        gather_words(0, 2)
+        multiply(0)
+        gather_bytes(1, 2)
+        gather_bytes(0, 2)
+        multiply(1)
+        turn(0)
+        first_layer(2, 1)
+        group_h(0)
+        first_layer(3, 0)
+        quantise_h(0)
+        turn(1)
+        silu(2)
+        second_layer(0)
+        gather_words(1, 2)
+        first_layer(3, 1)
+        group_h(1)
+        empty_y(0)
+        multiply(2)
+        quantise_h(1)
+        scatter(0, 0)
+        silu(3)
+        turn(2)
+        group_h(2)
+        multiply(3)
+        second_layer(1)
+        quantise_h(2)
+        empty_y(1)
+        scatter(0, 1)
+        turn(3)
+        group_h(3)
+        scatter(1, 0)
+        scatter(1, 1)
+        quantise_h(3)
+        second_layer(2)
+        scatter(0, 2)
+        empty_y(2)
+        scatter(1, 2)
+        second_layer(3)
+        empty_y(3)
+        scatter(2, 0)
+        scatter(2, 1)
+        scatter(2, 2)
+        scatter(3, 0)
+        scatter(3, 1)
+        scatter(3, 2)
+
+        for n in range(N_TILES):
+            nc.sync.dma_start(out[n * P : (n + 1) * P, :], out_sb[n][:])

@@ -19,13 +19,14 @@ MULT = mybir.AluOpType.mult
 P = 128
 PASSES = K // 512
 HALF = T // 2
-VECTOR_COLUMNS = ((192, 192), (0, 160))
 TILES = T // P
 N_TILES = N // P
-GROUPS = ((0, 128), (128, 384), (384, 512))
 
 FLOPS = 2 * T * (2 * K * H + H * N)
 BYTES = 4 * K * T + 2 * E * (K * H // 2 + K * H // 32) + E * (H * N // 2 + H * N // 32) + 4 * P * T + 2 * P * (T // 16) + 4 * N * T
+
+VECTOR_TOKENS = 176
+ORDER = (3, 2, 0, 1)
 
 
 def tile_moe_rag_glu_silu_kernel(
@@ -34,30 +35,23 @@ def tile_moe_rag_glu_silu_kernel(
     nc = tc.nc
     with ExitStack() as ctx:
         keep = ctx.enter_context(tc.tile_pool(name="keep", bufs=1))
-        work = ctx.enter_context(tc.tile_pool(name="work", bufs=3))
-        psum_ab = ctx.enter_context(tc.psum_pool(name="psum_ab", bufs=3))
-        psum_one = ctx.enter_context(tc.psum_pool(name="psum_one", bufs=1))
-
-        offsets = keep.tile([P, T // 16], U16, name="offsets")
+        psum = ctx.enter_context(tc.psum_pool(name="psum", bufs=1))
 
         def scale_plane(name, scales):
             plane = keep.tile([P, E * scales.shape[1], scales.shape[3]], U8, name=f"{name}_plane", align_bytes=64)
             nc.vector.memset(plane[:].bitcast(I32), 0)
             return plane
 
-        def load_scales(queue, plane, scales):
-            rows = scales.bitcast(I32).rearrange("e s q i -> q (e s) i")
-            for q in range(4):
-                queue.dma_start(plane[32 * q : 32 * q + 4, :, :].bitcast(I32), rows[4 * q : 4 * q + 4, :, :])
+        def load_scales(plane, scales):
+            rows = scales.bitcast(I32).rearrange("e s (g r) i -> r g (e s) i", r=4)
+            for r in range(4):
+                nc.sync.dma_start(plane[r:P:32, :, :].bitcast(I32), rows[r])
 
-        def load_x(s):
+        def load_x(s, half):
             rows = xT[s * 512 : (s + 1) * 512, :].rearrange("(p j) w -> p j w", j=4)
-            halves = []
-            for half in range(2):
-                raw = keep.tile([P, 4, HALF], F32, name=f"x_raw_{s}_{half}")
-                nc.sync.dma_start(raw[:], rows[:, :, half * HALF : (half + 1) * HALF])
-                halves.append(raw)
-            return halves
+            raw = keep.tile([P, 4, HALF], F32, name=f"x_raw_{s}_{half}")
+            nc.sync.dma_start(raw[:], rows[:, :, half * HALF : (half + 1) * HALF])
+            return raw
 
         def load_words(name, words, e):
             codes = keep.tile([P, words.shape[1], words.shape[3]], U8, name=f"{name}_codes_{e}", align_bytes=64)
@@ -67,25 +61,31 @@ def tile_moe_rag_glu_silu_kernel(
         w1_sc = scale_plane("w1", w1_scales)
         w3_sc = scale_plane("w3", w3_scales)
         w2_sc = scale_plane("w2", w2_scales)
-        all_bytes = []
+        all_words, all_bytes, slot_words, slot_bytes = [], [], [], []
         for s in range(PASSES):
-            plane = keep.tile([P, T], U8, name=f"all_bytes_{s}", align_bytes=64)
-            nc.vector.memset(plane[:].bitcast(I32), 0)
-            all_bytes.append(plane)
+            all_words.append(keep.tile([P, T], I32, name=f"all_words_{s}", align_bytes=64))
+            all_bytes.append(keep.tile([P, T], U8, name=f"all_bytes_{s}", align_bytes=64))
+            slot_words.append(keep.tile([P, T], U32, name=f"slot_words_{s}", align_bytes=64))
+            slot_bytes.append(keep.tile([P, T], U8, name=f"slot_bytes_{s}", align_bytes=64))
+            nc.vector.memset(all_bytes[s][:].bitcast(I32), 0)
+        nc.vector.memset(all_words[1][:, 0:HALF], 0)
 
-        x_raw = [load_x(0)]
+        offsets = keep.tile([P, T // 16], U16, name="offsets")
+        x_raw, w1, w3 = {}, {}, {}
+        x_raw[0, 1] = load_x(0, 1)
+        x_raw[0, 0] = load_x(0, 0)
         nc.sync.dma_start(offsets[:], offs)
-        load_scales(nc.sync, w1_sc, w1_scales)
-        x_raw.append(load_x(1))
-        load_scales(nc.sync, w3_sc, w3_scales)
-        w1, w3 = [], []
-        for e in range(E):
-            w1.append(load_words("w1", w1_words, e))
-            w3.append(load_words("w3", w3_words, e))
-        load_scales(nc.sync, w2_sc, w2_scales)
+        w1[1] = load_words("w1", w1_words, 1)
+        load_scales(w1_sc, w1_scales)
+        x_raw[1, 1] = load_x(1, 1)
+        x_raw[1, 0] = load_x(1, 0)
+        w3[1] = load_words("w3", w3_words, 1)
+        load_scales(w3_sc, w3_scales)
+        w1[0] = load_words("w1", w1_words, 0)
+        w3[0] = load_words("w3", w3_words, 0)
+        load_scales(w2_sc, w2_scales)
         w2 = keep.tile([P, E, 2 * N], U8, name="w2", align_bytes=64)
         nc.sync.dma_start(w2[:].bitcast(I32), w2_words.bitcast(I32)[:, 0].rearrange("e p b -> p e b"))
-
         gate_sb = keep.tile([P, T], F32, name="gate_sb")
         nc.sync.dma_start(gate_sb[:], gate[0:P, :])
 
@@ -97,113 +97,86 @@ def tile_moe_rag_glu_silu_kernel(
         warm_out = keep.tile([P, 1], F32, name="warm_out")
         nc.scalar.activation(warm_out[:], warm[:], ACT.Silu)
 
-        grouped, all_words, x_words, x_bytes = {}, [], [], []
-        for s in range(PASSES):
-            words = keep.tile([P, T], U32, name=f"all_words_{s}", align_bytes=64)
-            slot_words = keep.tile([P, T], U32, name=f"slot_words_{s}", align_bytes=64)
-            slot_bytes = keep.tile([P, T], U8, name=f"slot_bytes_{s}", align_bytes=64)
-            all_words.append(words)
-            x_words.append(slot_words)
-            x_bytes.append(slot_bytes)
-            for half in range(2):
-                tokens = keep.tile([P, HALF, 4], BF16, name=f"grouped_{s}_{half}", align_bytes=64)
-                grouped[s, half] = tokens
-        out_sb = []
-        for n in range(N_TILES):
-            window = keep.tile([P, T], F32, name=f"out_sb_{n}")
-            out_sb.append(window)
-        sums, acts, hidden, turned, h_grouped, h_codes, y_sums, y_sb = {}, {}, {}, {}, {}, {}, {}, {}
+        out_sb = [keep.tile([P, T], F32, name=f"out_sb_{n}") for n in range(N_TILES)]
+        bank_a = [psum.tile([P, H], F32, name=f"bank_a_{t}") for t in range(TILES)]
+        bank_b = [psum.tile([P, H], F32, name=f"bank_b_{t}") for t in range(TILES)]
+        acts, hidden, h_grouped, h_codes, y_sb = {}, {}, {}, {}, {}
 
-        def cast(engine_copy, s, half, lo, hi):
-            engine_copy(
-                grouped[s, half][:, lo:hi, :].rearrange("p (c i) j -> p c j i", i=4),
-                x_raw[s][half][:, :, lo:hi].rearrange("p j (c i) -> p c j i", i=4),
-            )
-
-        def cast_s(s, half):
-            cast(nc.scalar.copy, s, half, VECTOR_COLUMNS[s][half], HALF)
-
-        def cast_v(s, half):
-            cast(nc.vector.tensor_copy, s, half, 0, VECTOR_COLUMNS[s][half])
+        def expert_of(t):
+            return 0 if t == 0 else 1
 
         def quantise_x(s, half):
+            grouped = keep.tile([P, HALF, 4], BF16, name=f"grouped_{s}_{half}", align_bytes=64)
+            for copy, lo, hi in ((nc.scalar.copy, VECTOR_TOKENS, HALF), (nc.vector.tensor_copy, 0, VECTOR_TOKENS)):
+                copy(
+                    grouped[:, lo:hi, :].rearrange("p (c i) j -> p c j i", i=4),
+                    x_raw[s, half][:, :, lo:hi].rearrange("p j (c i) -> p c j i", i=4),
+                )
             cols = slice(half * HALF, (half + 1) * HALF)
             nc.vector.quantize_mx(
                 out=all_words[s][:, cols].bitcast(FP8X4),
                 scales=all_bytes[s][:, cols],
-                in_=grouped[s, half][:].rearrange("p w j -> p (w j)"),
+                in_=grouped[:].rearrange("p w j -> p (w j)"),
             )
 
-        def gather(picked, tokens, group):
-            lo, hi = GROUPS[group]
-            nc.vector.tensor_copy(picked[:, lo:hi], tokens[:].indirect(offsets[:, lo // 16 : hi // 16]))
+        def gather(s, lo, hi):
+            where = offsets[:, lo // 16 : hi // 16]
+            nc.vector.tensor_copy(slot_words[s][:, lo:hi], all_words[s][:].bitcast(U32).indirect(where))
+            nc.vector.tensor_copy(slot_bytes[s][:, lo:hi], all_bytes[s][:].indirect(where))
 
-        def gather_words(s, group):
-            gather(x_words[s], all_words[s], group)
-
-        def gather_bytes(s, group):
-            gather(x_bytes[s], all_bytes[s], group)
-
-        def first_layer(t, s):
-            e = 0 if t == 0 else 1
+        def first_layer(t, s, bank, codes, plane):
             cols = slice(t * P, (t + 1) * P)
-            if s == 0:
-                a = psum_ab.tile([P, H], F32, name="a")
-                b = psum_ab.tile([P, H], F32, name="b")
-                sums[t] = (a, b)
-            for acc, codes, plane in zip(sums[t], (w1, w3), (w1_sc, w3_sc)):
-                nc.tensor.matmul_mx(
-                    out=acc[:],
-                    lhsT=x_words[s][:, cols].bitcast(FP8X4),
-                    lhsT_scale=x_bytes[s][:, cols],
-                    rhs=codes[e][:, s, :].bitcast(FP4X4),
-                    rhs_scale=plane[:, PASSES * e + s, :],
-                    start=(s == 0),
-                    stop=(s == PASSES - 1),
-                )
+            e = expert_of(t)
+            nc.tensor.matmul_mx(
+                out=bank[t][:],
+                lhsT=slot_words[s][:, cols].bitcast(FP8X4),
+                lhsT_scale=slot_bytes[s][:, cols],
+                rhs=codes[e][:, s, :].bitcast(FP4X4),
+                rhs_scale=plane[:, PASSES * e + s, :],
+                start=(s == 0),
+                stop=(s == PASSES - 1),
+            )
+
+        def sum_a(t, s):
+            first_layer(t, s, bank_a, w1, w1_sc)
+
+        def sum_b(t, s):
+            first_layer(t, s, bank_b, w3, w3_sc)
 
         def silu(t):
-            act = work.tile([P, H], F32, name="act")
-            nc.scalar.activation(act[:], sums[t][0][:], ACT.Silu)
-            acts[t] = act
+            acts[t] = keep.tile([P, H], F32, name=f"act_{t}")
+            nc.scalar.activation(acts[t][:], bank_a[t][:], ACT.Silu)
 
         def multiply(t):
-            h = work.tile([P, 2, P, 2], BF16, name="h", align_bytes=64)
+            hidden[t] = keep.tile([P, 2, P, 2], BF16, name=f"h_{t}", align_bytes=64)
             nc.vector.tensor_tensor(
-                h[:],
+                hidden[t][:],
                 acts[t][:].rearrange("p (q u d) -> p u q d", u=2, d=2),
-                sums[t][1][:].rearrange("p (q u d) -> p u q d", u=2, d=2),
+                bank_b[t][:].rearrange("p (q u d) -> p u q d", u=2, d=2),
                 MULT,
             )
-            hidden[t] = h
 
         def turn(t):
-            bank = psum_one.tile([P, 2, P], F32, name="turned")
             pairs = hidden[t][:].rearrange("p u q d -> p (u q d)").bitcast(F32)
             for u in range(2):
-                nc.tensor.transpose(bank[:, u, :], pairs[:, u * P : (u + 1) * P], ident[:])
-            turned[t] = bank
-
-        def group_h(t):
-            h4 = work.tile([P, P, 4], BF16, name="h4", align_bytes=64)
-            nc.scalar.copy(h4[:].bitcast(F32), turned[t][:].rearrange("p u r -> p r u"))
-            h_grouped[t] = h4
+                nc.tensor.transpose(bank_a[t][:, u * P : (u + 1) * P], pairs[:, u * P : (u + 1) * P], ident[:])
+            h_grouped[t] = keep.tile([P, P, 4], BF16, name=f"h4_{t}", align_bytes=64)
+            nc.scalar.copy(h_grouped[t][:].bitcast(F32), bank_a[t][:, 0 : 2 * P].rearrange("p (u r) -> p r u", u=2))
 
         def quantise_h(t):
-            h_words = work.tile([P, P], U32, name="h_words", align_bytes=64)
-            h_bytes = work.tile([P, P], U8, name="h_bytes", align_bytes=64)
+            h_words = keep.tile([P, P], U32, name=f"h_words_{t}", align_bytes=64)
+            h_bytes = keep.tile([P, P], U8, name=f"h_bytes_{t}", align_bytes=64)
             nc.vector.quantize_mx(
                 out=h_words[:].bitcast(FP8X4), scales=h_bytes[:], in_=h_grouped[t][:].rearrange("p r j -> p (r j)")
             )
             h_codes[t] = (h_words, h_bytes)
 
         def second_layer(t):
-            e = 0 if t == 0 else 1
+            e = expert_of(t)
             h_words, h_bytes = h_codes[t]
-            y = psum_one.tile([P, N_TILES, P], F32, name="y")
             for n in range(N_TILES):
                 nc.tensor.matmul_mx(
-                    out=y[:, n, :],
+                    out=bank_b[t][:, n * P : (n + 1) * P],
                     lhsT=w2[:, e, 2 * P * n : 2 * P * (n + 1)].bitcast(FP4X4),
                     lhsT_scale=w2_sc[:, e, P * n : P * (n + 1)],
                     rhs=h_words[:].bitcast(FP8X4),
@@ -211,89 +184,65 @@ def tile_moe_rag_glu_silu_kernel(
                     start=True,
                     stop=True,
                 )
-            y_sums[t] = y
-
-        def empty_y(t):
-            result = work.tile([P, N_TILES, P], F32, name="result")
-            nc.scalar.copy(result[:], y_sums[t][:])
-            y_sb[t] = result
+            y_sb[t] = keep.tile([P, N], F32, name=f"y_{t}")
+            nc.scalar.copy(y_sb[t][:], bank_b[t][:, 0:N])
 
         def scatter(t, n):
-            cols = slice(t * P, (t + 1) * P)
             where = offsets[:, t * P // 16 : (t + 1) * P // 16]
-            nc.vector.tensor_tensor(out_sb[n][:].indirect(where), y_sb[t][:, n, :], gate_sb[:, cols], MULT)
+            nc.vector.tensor_tensor(
+                out_sb[n][:].indirect(where), y_sb[t][:, n * P : (n + 1) * P], gate_sb[:, t * P : (t + 1) * P], MULT
+            )
 
-        cast_s(0, 0)
-        cast_v(0, 0)
-        quantise_x(0, 0)
-        cast_s(0, 1)
-        cast_v(0, 1)
-        cast_s(1, 0)
+        first, second, third, last = ORDER
         quantise_x(0, 1)
-        gather_words(0, 0)
-        gather_words(0, 1)
-        cast_s(1, 1)
-        gather_bytes(0, 0)
-        cast_v(1, 1)
-        quantise_x(1, 0)
+        quantise_x(0, 0)
+        gather(0, 3 * P, T)
+        gather(0, 0, 3 * P)
+        for t in (first, second, last):
+            sum_a(t, 0)
         quantise_x(1, 1)
-        gather_bytes(0, 1)
-        gather_words(1, 0)
-        gather_bytes(1, 0)
-        first_layer(0, 0)
-        gather_bytes(1, 1)
-        first_layer(0, 1)
-        silu(0)
-        first_layer(1, 0)
-        gather_words(1, 1)
-        first_layer(1, 1)
-        silu(1)
-        first_layer(2, 0)
-        gather_words(0, 2)
-        multiply(0)
-        gather_bytes(1, 2)
-        gather_bytes(0, 2)
-        multiply(1)
-        turn(0)
-        first_layer(2, 1)
-        group_h(0)
-        first_layer(3, 0)
-        quantise_h(0)
-        turn(1)
-        silu(2)
-        second_layer(0)
-        gather_words(1, 2)
-        first_layer(3, 1)
-        group_h(1)
-        empty_y(0)
-        multiply(2)
-        quantise_h(1)
-        scatter(0, 0)
-        silu(3)
-        turn(2)
-        group_h(2)
-        multiply(3)
-        second_layer(1)
-        quantise_h(2)
-        empty_y(1)
-        scatter(0, 1)
-        turn(3)
-        group_h(3)
-        scatter(1, 0)
-        scatter(1, 1)
-        quantise_h(3)
-        second_layer(2)
-        scatter(0, 2)
-        empty_y(2)
-        scatter(1, 2)
-        second_layer(3)
-        empty_y(3)
-        scatter(2, 0)
-        scatter(2, 1)
-        scatter(2, 2)
-        scatter(3, 0)
-        scatter(3, 1)
-        scatter(3, 2)
-
+        gather(1, 3 * P, T)
+        sum_a(first, 1)
+        silu(first)
+        quantise_x(1, 0)
+        for s in range(PASSES):
+            sum_b(first, s)
+        for t in ORDER[1:]:
+            gather(1, t * P, (t + 1) * P)
+        multiply(first)
+        sum_a(second, 1)
+        silu(second)
+        for s in range(PASSES):
+            sum_b(second, s)
+        turn(first)
+        multiply(second)
+        for s in range(PASSES):
+            sum_a(third, s)
+        silu(third)
+        for s in range(PASSES):
+            sum_b(third, s)
+        quantise_h(first)
+        turn(second)
+        multiply(third)
+        sum_a(last, 1)
+        silu(last)
+        for s in range(PASSES):
+            sum_b(last, s)
+        second_layer(first)
+        quantise_h(second)
+        turn(third)
+        multiply(last)
+        second_layer(second)
+        quantise_h(third)
         for n in range(N_TILES):
+            scatter(first, n)
+        turn(last)
+        second_layer(third)
+        quantise_h(last)
+        for n in range(N_TILES):
+            scatter(second, n)
+        second_layer(last)
+        for n in range(N_TILES):
+            scatter(third, n)
+            scatter(last, n)
             nc.sync.dma_start(out[n * P : (n + 1) * P, :], out_sb[n][:])

@@ -25,7 +25,7 @@ N_TILES = N // P
 FLOPS = 2 * T * (2 * K * H + H * N)
 BYTES = 4 * K * T + 2 * E * (K * H // 2 + K * H // 32) + E * (H * N // 2 + H * N // 32) + 4 * P * T + 2 * P * (T // 16) + 4 * N * T
 
-VECTOR_TOKENS = 176
+VECTOR_TOKENS = ((128, 176), (0, 0))
 ORDER = (3, 2, 0, 1)
 
 
@@ -35,6 +35,8 @@ def tile_moe_rag_glu_silu_kernel(
     nc = tc.nc
     with ExitStack() as ctx:
         keep = ctx.enter_context(tc.tile_pool(name="keep", bufs=1))
+        tail = ctx.enter_context(tc.tile_pool(name="tail", bufs=1))
+        reuse = ctx.enter_context(tc.tile_pool(name="reuse", bufs=1))
         psum = ctx.enter_context(tc.psum_pool(name="psum", bufs=1))
 
         def scale_plane(name, scales):
@@ -61,28 +63,25 @@ def tile_moe_rag_glu_silu_kernel(
         w1_sc = scale_plane("w1", w1_scales)
         w3_sc = scale_plane("w3", w3_scales)
         w2_sc = scale_plane("w2", w2_scales)
-        all_words, all_bytes, slot_words, slot_bytes = [], [], [], []
+        all_words, all_bytes, slot_words, slot_bytes = [], [], {}, {}
         for s in range(PASSES):
             all_words.append(keep.tile([P, T], I32, name=f"all_words_{s}", align_bytes=64))
             all_bytes.append(keep.tile([P, T], U8, name=f"all_bytes_{s}", align_bytes=64))
-            slot_words.append(keep.tile([P, T], U32, name=f"slot_words_{s}", align_bytes=64))
-            slot_bytes.append(keep.tile([P, T], U8, name=f"slot_bytes_{s}", align_bytes=64))
             nc.vector.memset(all_bytes[s][:].bitcast(I32), 0)
-        nc.vector.memset(all_words[1][:, 0:HALF], 0)
+            nc.vector.memset(all_words[s][:, 0:HALF], 0)
 
         offsets = keep.tile([P, T // 16], U16, name="offsets")
         x_raw, w1, w3 = {}, {}, {}
         x_raw[0, 1] = load_x(0, 1)
         x_raw[0, 0] = load_x(0, 0)
         nc.sync.dma_start(offsets[:], offs)
-        w1[1] = load_words("w1", w1_words, 1)
         load_scales(w1_sc, w1_scales)
         x_raw[1, 1] = load_x(1, 1)
         x_raw[1, 0] = load_x(1, 0)
-        w3[1] = load_words("w3", w3_words, 1)
         load_scales(w3_sc, w3_scales)
-        w1[0] = load_words("w1", w1_words, 0)
-        w3[0] = load_words("w3", w3_words, 0)
+        for e in (1, 0):
+            w1[e] = load_words("w1", w1_words, e)
+            w3[e] = load_words("w3", w3_words, e)
         load_scales(w2_sc, w2_scales)
         w2 = keep.tile([P, E, 2 * N], U8, name="w2", align_bytes=64)
         nc.sync.dma_start(w2[:].bitcast(I32), w2_words.bitcast(I32)[:, 0].rearrange("e p b -> p e b"))
@@ -97,21 +96,23 @@ def tile_moe_rag_glu_silu_kernel(
         warm_out = keep.tile([P, 1], F32, name="warm_out")
         nc.scalar.activation(warm_out[:], warm[:], ACT.Silu)
 
-        out_sb = [keep.tile([P, T], F32, name=f"out_sb_{n}") for n in range(N_TILES)]
+        out_sb = {}
         bank_a = [psum.tile([P, H], F32, name=f"bank_a_{t}") for t in range(TILES)]
         bank_b = [psum.tile([P, H], F32, name=f"bank_b_{t}") for t in range(TILES)]
-        acts, hidden, h_grouped, h_codes, y_sb = {}, {}, {}, {}, {}
+        acts, hidden, h_grouped, h_codes = {}, {}, {}, {}
+        y_sb = keep.tile([P, N_TILES, T], F32, name="y_sb")
 
         def expert_of(t):
             return 0 if t == 0 else 1
 
         def quantise_x(s, half):
             grouped = keep.tile([P, HALF, 4], BF16, name=f"grouped_{s}_{half}", align_bytes=64)
-            for copy, lo, hi in ((nc.scalar.copy, VECTOR_TOKENS, HALF), (nc.vector.tensor_copy, 0, VECTOR_TOKENS)):
-                copy(
-                    grouped[:, lo:hi, :].rearrange("p (c i) j -> p c j i", i=4),
-                    x_raw[s, half][:, :, lo:hi].rearrange("p j (c i) -> p c j i", i=4),
-                )
+            for copy, lo, hi in ((nc.scalar.copy, VECTOR_TOKENS[s][half], HALF), (nc.vector.tensor_copy, 0, VECTOR_TOKENS[s][half])):
+                if hi > lo:
+                    copy(
+                        grouped[:, lo:hi, :].rearrange("p (c i) j -> p c j i", i=4),
+                        x_raw[s, half][:, :, lo:hi].rearrange("p j (c i) -> p c j i", i=4),
+                    )
             cols = slice(half * HALF, (half + 1) * HALF)
             nc.vector.quantize_mx(
                 out=all_words[s][:, cols].bitcast(FP8X4),
@@ -119,18 +120,26 @@ def tile_moe_rag_glu_silu_kernel(
                 in_=grouped[:].rearrange("p w j -> p (w j)"),
             )
 
-        def gather(s, lo, hi):
+        def gather(s, lo, hi, over_act=False):
+            if over_act:
+                words = reuse.tile([P, hi - lo], U32, name=f"slot_words_{s}_{lo}", align_bytes=64, offset=0)
+                scale_bytes = reuse.tile([P, hi - lo], U8, name=f"slot_bytes_{s}_{lo}", align_bytes=64, offset=4 * (hi - lo))
+            else:
+                words = keep.tile([P, hi - lo], U32, name=f"slot_words_{s}_{lo}", align_bytes=64)
+                scale_bytes = keep.tile([P, hi - lo], U8, name=f"slot_bytes_{s}_{lo}", align_bytes=64)
             where = offsets[:, lo // 16 : hi // 16]
-            nc.vector.tensor_copy(slot_words[s][:, lo:hi], all_words[s][:].bitcast(U32).indirect(where))
-            nc.vector.tensor_copy(slot_bytes[s][:, lo:hi], all_bytes[s][:].indirect(where))
+            nc.vector.tensor_copy(words[:], all_words[s][:].bitcast(U32).indirect(where))
+            nc.vector.tensor_copy(scale_bytes[:], all_bytes[s][:].indirect(where))
+            for t in range(lo // P, hi // P):
+                slot_words[s, t] = words[:, t * P - lo : (t + 1) * P - lo]
+                slot_bytes[s, t] = scale_bytes[:, t * P - lo : (t + 1) * P - lo]
 
         def first_layer(t, s, bank, codes, plane):
-            cols = slice(t * P, (t + 1) * P)
             e = expert_of(t)
             nc.tensor.matmul_mx(
                 out=bank[t][:],
-                lhsT=slot_words[s][:, cols].bitcast(FP8X4),
-                lhsT_scale=slot_bytes[s][:, cols],
+                lhsT=slot_words[s, t].bitcast(FP8X4),
+                lhsT_scale=slot_bytes[s, t],
                 rhs=codes[e][:, s, :].bitcast(FP4X4),
                 rhs_scale=plane[:, PASSES * e + s, :],
                 start=(s == 0),
@@ -144,7 +153,10 @@ def tile_moe_rag_glu_silu_kernel(
             first_layer(t, s, bank_b, w3, w3_sc)
 
         def silu(t):
-            acts[t] = keep.tile([P, H], F32, name=f"act_{t}")
+            if t == ORDER[0]:
+                acts[t] = reuse.tile([P, H], F32, name=f"act_{t}", align_bytes=64, offset=0)
+            else:
+                acts[t] = keep.tile([P, H], F32, name=f"act_{t}")
             nc.scalar.activation(acts[t][:], bank_a[t][:], ACT.Silu)
 
         def multiply(t):
@@ -160,7 +172,10 @@ def tile_moe_rag_glu_silu_kernel(
             pairs = hidden[t][:].rearrange("p u q d -> p (u q d)").bitcast(F32)
             for u in range(2):
                 nc.tensor.transpose(bank_a[t][:, u * P : (u + 1) * P], pairs[:, u * P : (u + 1) * P], ident[:])
-            h_grouped[t] = keep.tile([P, P, 4], BF16, name=f"h4_{t}", align_bytes=64)
+            if t == ORDER[-1]:
+                h_grouped[t] = tail.tile([P, P, 4], BF16, name=f"h4_{t}", align_bytes=64, offset=2 * 4 * T - 4 * P)
+            else:
+                h_grouped[t] = keep.tile([P, P, 4], BF16, name=f"h4_{t}", align_bytes=64)
             nc.scalar.copy(h_grouped[t][:].bitcast(F32), bank_a[t][:, 0 : 2 * P].rearrange("p (u r) -> p r u", u=2))
 
         def quantise_h(t):
@@ -184,65 +199,37 @@ def tile_moe_rag_glu_silu_kernel(
                     start=True,
                     stop=True,
                 )
-            y_sb[t] = keep.tile([P, N], F32, name=f"y_{t}")
-            nc.scalar.copy(y_sb[t][:], bank_b[t][:, 0:N])
+            nc.scalar.copy(y_sb[:, :, t * P : (t + 1) * P], bank_b[t][:, 0:N].rearrange("p (n r) -> p n r", n=N_TILES))
 
-        def scatter(t, n):
-            where = offsets[:, t * P // 16 : (t + 1) * P // 16]
-            nc.vector.tensor_tensor(
-                out_sb[n][:].indirect(where), y_sb[t][:, n * P : (n + 1) * P], gate_sb[:, t * P : (t + 1) * P], MULT
-            )
+        def scatter(lo, hi, n):
+            if n not in out_sb:
+                out_sb[n] = tail.tile([P, T], F32, name=f"out_sb_{n}", offset=n * 4 * T)
+            where = offsets[:, lo // 16 : hi // 16]
+            nc.vector.tensor_tensor(out_sb[n][:].indirect(where), y_sb[:, n, lo:hi], gate_sb[:, lo:hi], MULT)
 
         first, second, third, last = ORDER
         quantise_x(0, 1)
-        quantise_x(0, 0)
         gather(0, 3 * P, T)
+        quantise_x(0, 0)
         gather(0, 0, 3 * P)
-        for t in (first, second, last):
-            sum_a(t, 0)
         quantise_x(1, 1)
         gather(1, 3 * P, T)
-        sum_a(first, 1)
-        silu(first)
         quantise_x(1, 0)
-        for s in range(PASSES):
-            sum_b(first, s)
-        for t in ORDER[1:]:
-            gather(1, t * P, (t + 1) * P)
-        multiply(first)
-        sum_a(second, 1)
-        silu(second)
-        for s in range(PASSES):
-            sum_b(second, s)
-        turn(first)
-        multiply(second)
-        for s in range(PASSES):
-            sum_a(third, s)
-        silu(third)
-        for s in range(PASSES):
-            sum_b(third, s)
-        quantise_h(first)
-        turn(second)
-        multiply(third)
-        sum_a(last, 1)
-        silu(last)
-        for s in range(PASSES):
-            sum_b(last, s)
-        second_layer(first)
-        quantise_h(second)
-        turn(third)
-        multiply(last)
-        second_layer(second)
-        quantise_h(third)
+        gather(1, 2 * P, 3 * P)
+        gather(1, 0, 2 * P)
+        for t in ORDER:
+            for s in range(PASSES):
+                sum_a(t, s)
+            silu(t)
+            for s in range(PASSES):
+                sum_b(t, s)
+            multiply(t)
+        for t in ORDER:
+            turn(t)
+            quantise_h(t)
+            second_layer(t)
+        for lo, hi in ((3 * P, T), (2 * P, 3 * P), (0, 2 * P)):
+            for n in range(N_TILES):
+                scatter(lo, hi, n)
         for n in range(N_TILES):
-            scatter(first, n)
-        turn(last)
-        second_layer(third)
-        quantise_h(last)
-        for n in range(N_TILES):
-            scatter(second, n)
-        second_layer(last)
-        for n in range(N_TILES):
-            scatter(third, n)
-            scatter(last, n)
             nc.sync.dma_start(out[n * P : (n + 1) * P, :], out_sb[n][:])

@@ -25,8 +25,8 @@ N_TILES = N // P
 FLOPS = 2 * T * (2 * K * H + H * N)
 BYTES = 4 * K * T + 2 * E * (K * H // 2 + K * H // 32) + E * (H * N // 2 + H * N // 32) + 4 * P * T + 2 * P * (T // 16) + 4 * N * T
 
-VECTOR_TOKENS = ((128, 176), (0, 0))
-ORDER = (3, 2, 0, 1)
+VECTOR_TOKENS = ((64, 176), (0, 0))
+ORDER = (3, 0, 1, 2)
 
 
 def tile_moe_rag_glu_silu_kernel(
@@ -173,7 +173,7 @@ def tile_moe_rag_glu_silu_kernel(
             for u in range(2):
                 nc.tensor.transpose(bank_a[t][:, u * P : (u + 1) * P], pairs[:, u * P : (u + 1) * P], ident[:])
             if t == ORDER[-1]:
-                h_grouped[t] = tail.tile([P, P, 4], BF16, name=f"h4_{t}", align_bytes=64, offset=2 * 4 * T - 4 * P)
+                h_grouped[t] = tail.tile([P, P, 4], BF16, name=f"h4_{t}", align_bytes=64, offset=2 * 4 * T)
             else:
                 h_grouped[t] = keep.tile([P, P, 4], BF16, name=f"h4_{t}", align_bytes=64)
             nc.scalar.copy(h_grouped[t][:].bitcast(F32), bank_a[t][:, 0 : 2 * P].rearrange("p (u r) -> p r u", u=2))
@@ -215,20 +215,24 @@ def tile_moe_rag_glu_silu_kernel(
         quantise_x(1, 1)
         gather(1, 3 * P, T)
         quantise_x(1, 0)
-        gather(1, 2 * P, 3 * P)
-        gather(1, 0, 2 * P)
-        for t in ORDER:
-            for s in range(PASSES):
-                sum_a(t, s)
-            silu(t)
-            for s in range(PASSES):
-                sum_b(t, s)
-            multiply(t)
-        for t in ORDER:
-            turn(t)
-            quantise_h(t)
-            second_layer(t)
-        for lo, hi in ((3 * P, T), (2 * P, 3 * P), (0, 2 * P)):
+        gather(1, 0, 3 * P)
+        for step in range(TILES + 2):
+            if step < TILES:
+                for s in range(PASSES):
+                    sum_a(ORDER[step], s)
+                silu(ORDER[step])
+            if 2 <= step:
+                second_layer(ORDER[step - 2])
+            if step < TILES:
+                for s in range(PASSES):
+                    sum_b(ORDER[step], s)
+            if 1 <= step <= TILES:
+                turn(ORDER[step - 1])
+            if step < TILES:
+                multiply(ORDER[step])
+            if 1 <= step <= TILES:
+                quantise_h(ORDER[step - 1])
+        for lo, hi in ((t * P, (t + 1) * P) for t in ORDER):
             for n in range(N_TILES):
                 scatter(lo, hi, n)
         for n in range(N_TILES):

@@ -25,7 +25,7 @@ N_TILES = N // P
 FLOPS = 2 * T * (2 * K * H + H * N)
 BYTES = 4 * K * T + 2 * E * (K * H // 2 + K * H // 32) + E * (H * N // 2 + H * N // 32) + 4 * P * T + 2 * P * (T // 16) + 4 * N * T
 
-VECTOR_TOKENS = ((64, 176), (0, 0))
+VECTOR_TOKENS = ((64, 176), (64, 0))
 ORDER = (3, 0, 1, 2)
 
 
@@ -55,10 +55,11 @@ def tile_moe_rag_glu_silu_kernel(
             nc.sync.dma_start(raw[:], rows[:, :, half * HALF : (half + 1) * HALF])
             return raw
 
-        def load_words(name, words, e):
-            codes = keep.tile([P, words.shape[1], words.shape[3]], U8, name=f"{name}_codes_{e}", align_bytes=64)
-            nc.sync.dma_start(codes[:].bitcast(I32), words.bitcast(I32)[e].rearrange("s p b -> p s b"))
-            return codes
+        def load_words(name, held, words, e, lo, hi):
+            codes = keep.tile([P, hi - lo, words.shape[3]], U8, name=f"{name}_codes_{e}_{lo}", align_bytes=64)
+            nc.sync.dma_start(codes[:].bitcast(I32), words.bitcast(I32)[e, lo:hi].rearrange("s p b -> p s b"))
+            for s in range(lo, hi):
+                held[e, s] = codes[:, s - lo, :]
 
         w1_sc = scale_plane("w1", w1_scales)
         w3_sc = scale_plane("w3", w3_scales)
@@ -76,12 +77,14 @@ def tile_moe_rag_glu_silu_kernel(
         x_raw[0, 0] = load_x(0, 0)
         nc.sync.dma_start(offsets[:], offs)
         load_scales(w1_sc, w1_scales)
+        load_words("w1", w1, w1_words, 1, 0, 1)
         x_raw[1, 1] = load_x(1, 1)
         x_raw[1, 0] = load_x(1, 0)
         load_scales(w3_sc, w3_scales)
-        for e in (1, 0):
-            w1[e] = load_words("w1", w1_words, e)
-            w3[e] = load_words("w3", w3_words, e)
+        load_words("w3", w3, w3_words, 1, 0, 2)
+        load_words("w1", w1, w1_words, 1, 1, 2)
+        load_words("w1", w1, w1_words, 0, 0, 2)
+        load_words("w3", w3, w3_words, 0, 0, 2)
         load_scales(w2_sc, w2_scales)
         w2 = keep.tile([P, E, 2 * N], U8, name="w2", align_bytes=64)
         nc.sync.dma_start(w2[:].bitcast(I32), w2_words.bitcast(I32)[:, 0].rearrange("e p b -> p e b"))
@@ -140,7 +143,7 @@ def tile_moe_rag_glu_silu_kernel(
                 out=bank[t][:],
                 lhsT=slot_words[s, t].bitcast(FP8X4),
                 lhsT_scale=slot_bytes[s, t],
-                rhs=codes[e][:, s, :].bitcast(FP4X4),
+                rhs=codes[e, s].bitcast(FP4X4),
                 rhs_scale=plane[:, PASSES * e + s, :],
                 start=(s == 0),
                 stop=(s == PASSES - 1),
@@ -216,9 +219,12 @@ def tile_moe_rag_glu_silu_kernel(
         gather(1, 3 * P, T)
         quantise_x(1, 0)
         gather(1, 0, 3 * P)
+        for t in ORDER:
+            if expert_of(t) == 1:
+                sum_a(t, 0)
         for step in range(TILES + 2):
             if step < TILES:
-                for s in range(PASSES):
+                for s in range(expert_of(ORDER[step]), PASSES):
                     sum_a(ORDER[step], s)
                 silu(ORDER[step])
             if 2 <= step:

@@ -94,11 +94,6 @@ def tile_moe_rag_glu_silu_kernel(
         ident = keep.tile([P, P], F32, name="ident")
         make_identity(nc, ident[:])
 
-        warm = keep.tile([P, 1], F32, name="warm")
-        nc.vector.memset(warm[:], 0.0)
-        warm_out = keep.tile([P, 1], F32, name="warm_out")
-        nc.scalar.activation(warm_out[:], warm[:], ACT.Silu)
-
         out_sb = {}
         bank_a = [psum.tile([P, H], F32, name=f"bank_a_{t}") for t in range(TILES)]
         bank_b = [psum.tile([P, H], F32, name=f"bank_b_{t}") for t in range(TILES)]

@@ -26,7 +26,7 @@ FLOPS = 2 * T * (2 * K * H + H * N)
 BYTES = 4 * K * T + 2 * E * (K * H // 2 + K * H // 32) + E * (H * N // 2 + H * N // 32) + 4 * P * T + 2 * P * (T // 16) + 4 * N * T
 
 VECTOR_TOKENS = ((64, 176), (64, 0))
-ORDER = (3, 0, 1, 2)
+ORDER = (3, 2, 0, 1)
 
 
 def tile_moe_rag_glu_silu_kernel(
@@ -61,6 +61,10 @@ def tile_moe_rag_glu_silu_kernel(
             for s in range(lo, hi):
                 held[e, s] = codes[:, s - lo, :]
 
+        warm = keep.tile([P, 2], F32, name="warm")
+        nc.vector.memset(warm[:, 0:1], 0.0)
+        nc.scalar.activation(warm[:, 1:2], warm[:, 0:1], ACT.Silu)
+
         w1_sc = scale_plane("w1", w1_scales)
         w3_sc = scale_plane("w3", w3_scales)
         w2_sc = scale_plane("w2", w2_scales)
@@ -81,8 +85,9 @@ def tile_moe_rag_glu_silu_kernel(
         x_raw[1, 1] = load_x(1, 1)
         x_raw[1, 0] = load_x(1, 0)
         load_scales(w3_sc, w3_scales)
-        load_words("w3", w3, w3_words, 1, 0, 2)
+        load_words("w3", w3, w3_words, 1, 0, 1)
         load_words("w1", w1, w1_words, 1, 1, 2)
+        load_words("w3", w3, w3_words, 1, 1, 2)
         load_words("w1", w1, w1_words, 0, 0, 2)
         load_words("w3", w3, w3_words, 0, 0, 2)
         load_scales(w2_sc, w2_scales)
@@ -118,19 +123,24 @@ def tile_moe_rag_glu_silu_kernel(
                 in_=grouped[:].rearrange("p w j -> p (w j)"),
             )
 
-        def gather(s, lo, hi, over_act=False):
-            if over_act:
+        def gather_words(s, lo, hi, over=False):
+            if over:
                 words = reuse.tile([P, hi - lo], U32, name=f"slot_words_{s}_{lo}", align_bytes=64, offset=0)
-                scale_bytes = reuse.tile([P, hi - lo], U8, name=f"slot_bytes_{s}_{lo}", align_bytes=64, offset=4 * (hi - lo))
             else:
                 words = keep.tile([P, hi - lo], U32, name=f"slot_words_{s}_{lo}", align_bytes=64)
-                scale_bytes = keep.tile([P, hi - lo], U8, name=f"slot_bytes_{s}_{lo}", align_bytes=64)
-            where = offsets[:, lo // 16 : hi // 16]
-            nc.vector.tensor_copy(words[:], all_words[s][:].bitcast(U32).indirect(where))
-            nc.vector.tensor_copy(scale_bytes[:], all_bytes[s][:].indirect(where))
+            nc.vector.tensor_copy(words[:], all_words[s][:].bitcast(U32).indirect(offsets[:, lo // 16 : hi // 16]))
             for t in range(lo // P, hi // P):
                 slot_words[s, t] = words[:, t * P - lo : (t + 1) * P - lo]
+
+        def gather_bytes(s, lo, hi):
+            scale_bytes = keep.tile([P, hi - lo], U8, name=f"slot_bytes_{s}_{lo}", align_bytes=64)
+            nc.vector.tensor_copy(scale_bytes[:], all_bytes[s][:].indirect(offsets[:, lo // 16 : hi // 16]))
+            for t in range(lo // P, hi // P):
                 slot_bytes[s, t] = scale_bytes[:, t * P - lo : (t + 1) * P - lo]
+
+        def gather(s, lo, hi, over=False):
+            gather_words(s, lo, hi, over)
+            gather_bytes(s, lo, hi)
 
         def first_layer(t, s, bank, codes, plane):
             e = expert_of(t)
@@ -151,10 +161,7 @@ def tile_moe_rag_glu_silu_kernel(
             first_layer(t, s, bank_b, w3, w3_sc)
 
         def silu(t):
-            if t == ORDER[0]:
-                acts[t] = reuse.tile([P, H], F32, name=f"act_{t}", align_bytes=64, offset=0)
-            else:
-                acts[t] = keep.tile([P, H], F32, name=f"act_{t}")
+            acts[t] = keep.tile([P, H], F32, name=f"act_{t}")
             nc.scalar.activation(acts[t][:], bank_a[t][:], ACT.Silu)
 
         def multiply(t):
@@ -205,34 +212,53 @@ def tile_moe_rag_glu_silu_kernel(
             where = offsets[:, lo // 16 : hi // 16]
             nc.vector.tensor_tensor(out_sb[n][:].indirect(where), y_sb[:, n, lo:hi], gate_sb[:, lo:hi], MULT)
 
-        first, second, third, last = ORDER
         quantise_x(0, 1)
         gather(0, 3 * P, T)
         quantise_x(0, 0)
-        gather(0, 0, 3 * P)
+        gather(0, 2 * P, 3 * P)
+        gather(0, 0, 2 * P)
         quantise_x(1, 1)
-        gather(1, 3 * P, T)
+        gather(1, 3 * P, T, over=True)
         quantise_x(1, 0)
-        gather(1, 0, 3 * P)
-        for t in ORDER:
-            if expert_of(t) == 1:
-                sum_a(t, 0)
-        for step in range(TILES + 2):
-            if step < TILES:
-                for s in range(expert_of(ORDER[step]), PASSES):
-                    sum_a(ORDER[step], s)
-                silu(ORDER[step])
-            if 2 <= step:
-                second_layer(ORDER[step - 2])
-            if step < TILES:
-                for s in range(PASSES):
-                    sum_b(ORDER[step], s)
-            if 1 <= step <= TILES:
-                turn(ORDER[step - 1])
-            if step < TILES:
-                multiply(ORDER[step])
-            if 1 <= step <= TILES:
-                quantise_h(ORDER[step - 1])
+        gather(1, 2 * P, 3 * P)
+        gather_bytes(1, 0, 2 * P)
+        sum_a(3, 0)
+        sum_a(2, 0)
+        sum_a(1, 0)
+        sum_b(3, 0)
+        sum_a(3, 1)
+        silu(3)
+        sum_b(3, 1)
+        multiply(3)
+        gather_words(1, 0, 2 * P, over=True)
+        turn(3)
+        quantise_h(3)
+        sum_b(2, 0)
+        sum_b(1, 0)
+        sum_a(2, 1)
+        silu(2)
+        sum_b(2, 1)
+        multiply(2)
+        second_layer(3)
+        sum_a(0, 0)
+        sum_b(0, 0)
+        sum_a(0, 1)
+        silu(0)
+        sum_b(0, 1)
+        turn(2)
+        quantise_h(2)
+        multiply(0)
+        sum_a(1, 1)
+        silu(1)
+        sum_b(1, 1)
+        second_layer(2)
+        turn(0)
+        multiply(1)
+        quantise_h(0)
+        turn(1)
+        second_layer(0)
+        quantise_h(1)
+        second_layer(1)
         for lo, hi in ((t * P, (t + 1) * P) for t in ORDER):
             for n in range(N_TILES):
                 scatter(lo, hi, n)

@@ -25,8 +25,8 @@ N_TILES = N // P
 FLOPS = 2 * T * (2 * K * H + H * N)
 BYTES = 4 * K * T + 2 * E * (K * H // 2 + K * H // 32) + E * (H * N // 2 + H * N // 32) + 4 * P * T + 2 * P * (T // 16) + 4 * N * T
 
-VECTOR_TOKENS = ((64, 176), (64, 0))
-ORDER = (3, 2, 0, 1)
+VECTOR_TOKENS = ((64, 176), (0, 112))
+ORDER = (3, 2, 1, 0)
 
 
 def tile_moe_rag_glu_silu_kernel(
@@ -49,10 +49,10 @@ def tile_moe_rag_glu_silu_kernel(
             for r in range(4):
                 nc.sync.dma_start(plane[r:P:32, :, :].bitcast(I32), rows[r])
 
-        def load_x(s, half):
+        def load_x(s):
             rows = xT[s * 512 : (s + 1) * 512, :].rearrange("(p j) w -> p j w", j=4)
-            raw = keep.tile([P, 4, HALF], F32, name=f"x_raw_{s}_{half}")
-            nc.sync.dma_start(raw[:], rows[:, :, half * HALF : (half + 1) * HALF])
+            raw = keep.tile([P, 4, T], F32, name=f"x_raw_{s}")
+            nc.sync.dma_start(raw[:], rows)
             return raw
 
         def load_words(name, held, words, e, lo, hi):
@@ -77,13 +77,11 @@ def tile_moe_rag_glu_silu_kernel(
 
         offsets = keep.tile([P, T // 16], U16, name="offsets")
         x_raw, w1, w3 = {}, {}, {}
-        x_raw[0, 1] = load_x(0, 1)
-        x_raw[0, 0] = load_x(0, 0)
+        x_raw[0] = load_x(0)
         nc.sync.dma_start(offsets[:], offs)
         load_scales(w1_sc, w1_scales)
         load_words("w1", w1, w1_words, 1, 0, 1)
-        x_raw[1, 1] = load_x(1, 1)
-        x_raw[1, 0] = load_x(1, 0)
+        x_raw[1] = load_x(1)
         load_scales(w3_sc, w3_scales)
         load_words("w3", w3, w3_words, 1, 0, 1)
         load_words("w1", w1, w1_words, 1, 1, 2)
@@ -114,7 +112,7 @@ def tile_moe_rag_glu_silu_kernel(
                 if hi > lo:
                     copy(
                         grouped[:, lo:hi, :].rearrange("p (c i) j -> p c j i", i=4),
-                        x_raw[s, half][:, :, lo:hi].rearrange("p j (c i) -> p c j i", i=4),
+                        x_raw[s][:, :, half * HALF + lo : half * HALF + hi].rearrange("p j (c i) -> p c j i", i=4),
                     )
             cols = slice(half * HALF, (half + 1) * HALF)
             nc.vector.quantize_mx(
@@ -204,7 +202,12 @@ def tile_moe_rag_glu_silu_kernel(
                     start=True,
                     stop=True,
                 )
-            nc.scalar.copy(y_sb[:, :, t * P : (t + 1) * P], bank_b[t][:, 0:N].rearrange("p (n r) -> p n r", n=N_TILES))
+            step = 1 if t == ORDER[-1] else N_TILES
+            for n in range(0, N_TILES, step):
+                nc.scalar.copy(
+                    y_sb[:, n : n + step, t * P : (t + 1) * P],
+                    bank_b[t][:, n * P : (n + step) * P].rearrange("p (n r) -> p n r", n=step),
+                )
 
         def scatter(lo, hi, n):
             if n not in out_sb:
@@ -215,13 +218,13 @@ def tile_moe_rag_glu_silu_kernel(
         quantise_x(0, 1)
         gather(0, 3 * P, T)
         quantise_x(0, 0)
-        gather(0, 2 * P, 3 * P)
-        gather(0, 0, 2 * P)
+        gather(0, P, 3 * P)
+        gather(0, 0, P)
         quantise_x(1, 1)
-        gather(1, 3 * P, T, over=True)
+        gather(1, 3 * P, T)
         quantise_x(1, 0)
         gather(1, 2 * P, 3 * P)
-        gather_bytes(1, 0, 2 * P)
+        gather(1, 0, 2 * P)
         sum_a(3, 0)
         sum_a(2, 0)
         sum_a(1, 0)
@@ -230,35 +233,34 @@ def tile_moe_rag_glu_silu_kernel(
         silu(3)
         sum_b(3, 1)
         multiply(3)
-        gather_words(1, 0, 2 * P, over=True)
-        turn(3)
-        quantise_h(3)
         sum_b(2, 0)
         sum_b(1, 0)
         sum_a(2, 1)
         silu(2)
         sum_b(2, 1)
         multiply(2)
-        second_layer(3)
-        sum_a(0, 0)
-        sum_b(0, 0)
-        sum_a(0, 1)
-        silu(0)
-        sum_b(0, 1)
-        turn(2)
-        quantise_h(2)
-        multiply(0)
+        turn(3)
+        quantise_h(3)
         sum_a(1, 1)
         silu(1)
         sum_b(1, 1)
-        second_layer(2)
-        turn(0)
         multiply(1)
-        quantise_h(0)
+        second_layer(3)
+        turn(2)
+        quantise_h(2)
+        sum_a(0, 0)
+        sum_a(0, 1)
+        silu(0)
+        sum_b(0, 0)
+        sum_b(0, 1)
+        multiply(0)
+        second_layer(2)
         turn(1)
-        second_layer(0)
         quantise_h(1)
+        turn(0)
         second_layer(1)
+        quantise_h(0)
+        second_layer(0)
         for lo, hi in ((t * P, (t + 1) * P) for t in ORDER):
             for n in range(N_TILES):
                 scatter(lo, hi, n)

@@ -25,8 +25,8 @@ N_TILES = N // P
 FLOPS = 2 * T * (2 * K * H + H * N)
 BYTES = 4 * K * T + 2 * E * (K * H // 2 + K * H // 32) + E * (H * N // 2 + H * N // 32) + 4 * P * T + 2 * P * (T // 16) + 4 * N * T
 
-VECTOR_TOKENS = ((64, 176), (0, 112))
-ORDER = (3, 2, 1, 0)
+VECTOR_TOKENS = ((64, 256), (48, 160))
+ORDER = (3, 2, 0, 1)
 
 
 def tile_moe_rag_glu_silu_kernel(
@@ -35,7 +35,6 @@ def tile_moe_rag_glu_silu_kernel(
     nc = tc.nc
     with ExitStack() as ctx:
         keep = ctx.enter_context(tc.tile_pool(name="keep", bufs=1))
-        tail = ctx.enter_context(tc.tile_pool(name="tail", bufs=1))
         reuse = ctx.enter_context(tc.tile_pool(name="reuse", bufs=1))
         psum = ctx.enter_context(tc.psum_pool(name="psum", bufs=1))
 
@@ -73,7 +72,8 @@ def tile_moe_rag_glu_silu_kernel(
             all_words.append(keep.tile([P, T], I32, name=f"all_words_{s}", align_bytes=64))
             all_bytes.append(keep.tile([P, T], U8, name=f"all_bytes_{s}", align_bytes=64))
             nc.vector.memset(all_bytes[s][:].bitcast(I32), 0)
-            nc.vector.memset(all_words[s][:, 0:HALF], 0)
+
+        nc.vector.memset(all_words[1][:, 0:HALF], 0)
 
         offsets = keep.tile([P, T // 16], U16, name="offsets")
         x_raw, w1, w3 = {}, {}, {}
@@ -97,28 +97,37 @@ def tile_moe_rag_glu_silu_kernel(
         ident = keep.tile([P, P], F32, name="ident")
         make_identity(nc, ident[:])
 
-        out_sb = {}
+        out_sb = [keep.tile([P, T], F32, name=f"out_sb_{n}") for n in range(N_TILES)]
+        low_sb = [keep.tile([P, HALF], F32, name=f"low_sb_{n}") for n in range(N_TILES)]
+        for n in range(N_TILES):
+            nc.vector.memset(out_sb[n][:, 0:HALF], 0.0)
         bank_a = [psum.tile([P, H], F32, name=f"bank_a_{t}") for t in range(TILES)]
         bank_b = [psum.tile([P, H], F32, name=f"bank_b_{t}") for t in range(TILES)]
-        acts, hidden, h_grouped, h_codes = {}, {}, {}, {}
-        y_sb = keep.tile([P, N_TILES, T], F32, name="y_sb")
+        acts, hidden, h_grouped, h_codes, grouped = {}, {}, {}, {}, {}
+        y_sb = {(t, n): keep.tile([P, P], F32, name=f"y_{t}_{n}") for n in range(N_TILES) for t in ORDER[-1:]}
+        for t in ORDER[:-1]:
+            y_sb[t] = keep.tile([P, N], F32, name=f"y_{t}")
+            for n in range(N_TILES):
+                y_sb[t, n] = y_sb[t][:, n * P : (n + 1) * P]
 
         def expert_of(t):
             return 0 if t == 0 else 1
 
-        def quantise_x(s, half):
-            grouped = keep.tile([P, HALF, 4], BF16, name=f"grouped_{s}_{half}", align_bytes=64)
+        def cast_x(s, half):
+            grouped[s, half] = keep.tile([P, HALF, 4], BF16, name=f"grouped_{s}_{half}", align_bytes=64)
             for copy, lo, hi in ((nc.scalar.copy, VECTOR_TOKENS[s][half], HALF), (nc.vector.tensor_copy, 0, VECTOR_TOKENS[s][half])):
                 if hi > lo:
                     copy(
-                        grouped[:, lo:hi, :].rearrange("p (c i) j -> p c j i", i=4),
+                        grouped[s, half][:, lo:hi, :].rearrange("p (c i) j -> p c j i", i=4),
                         x_raw[s][:, :, half * HALF + lo : half * HALF + hi].rearrange("p j (c i) -> p c j i", i=4),
                     )
+
+        def quantise_x(s, half):
             cols = slice(half * HALF, (half + 1) * HALF)
             nc.vector.quantize_mx(
                 out=all_words[s][:, cols].bitcast(FP8X4),
                 scales=all_bytes[s][:, cols],
-                in_=grouped[:].rearrange("p w j -> p (w j)"),
+                in_=grouped[s, half][:].rearrange("p w j -> p (w j)"),
             )
 
         def gather_words(s, lo, hi, over=False):
@@ -175,10 +184,7 @@ def tile_moe_rag_glu_silu_kernel(
             pairs = hidden[t][:].rearrange("p u q d -> p (u q d)").bitcast(F32)
             for u in range(2):
                 nc.tensor.transpose(bank_a[t][:, u * P : (u + 1) * P], pairs[:, u * P : (u + 1) * P], ident[:])
-            if t == ORDER[-1]:
-                h_grouped[t] = tail.tile([P, P, 4], BF16, name=f"h4_{t}", align_bytes=64, offset=2 * 4 * T)
-            else:
-                h_grouped[t] = keep.tile([P, P, 4], BF16, name=f"h4_{t}", align_bytes=64)
+            h_grouped[t] = keep.tile([P, P, 4], BF16, name=f"h4_{t}", align_bytes=64)
             nc.scalar.copy(h_grouped[t][:].bitcast(F32), bank_a[t][:, 0 : 2 * P].rearrange("p (u r) -> p r u", u=2))
 
         def quantise_h(t):
@@ -202,29 +208,31 @@ def tile_moe_rag_glu_silu_kernel(
                     start=True,
                     stop=True,
                 )
-            step = 1 if t == ORDER[-1] else N_TILES
-            for n in range(0, N_TILES, step):
-                nc.scalar.copy(
-                    y_sb[:, n : n + step, t * P : (t + 1) * P],
-                    bank_b[t][:, n * P : (n + step) * P].rearrange("p (n r) -> p n r", n=step),
-                )
+            if t == ORDER[-1]:
+                for n in range(N_TILES):
+                    nc.scalar.copy(y_sb[t, n][:], bank_b[t][:, n * P : (n + 1) * P])
+            else:
+                nc.scalar.copy(y_sb[t][:], bank_b[t][:, 0:N])
 
-        def scatter(lo, hi, n):
-            if n not in out_sb:
-                out_sb[n] = tail.tile([P, T], F32, name=f"out_sb_{n}", offset=n * 4 * T)
+        def scatter(window, t, n):
+            lo, hi = t * P, (t + 1) * P
             where = offsets[:, lo // 16 : hi // 16]
-            nc.vector.tensor_tensor(out_sb[n][:].indirect(where), y_sb[:, n, lo:hi], gate_sb[:, lo:hi], MULT)
+            nc.vector.tensor_tensor(window[:].indirect(where), y_sb[t, n][:], gate_sb[:, lo:hi], MULT)
 
+        cast_x(0, 1)
+        cast_x(0, 0)
         quantise_x(0, 1)
-        gather(0, 3 * P, T)
         quantise_x(0, 0)
-        gather(0, P, 3 * P)
-        gather(0, 0, P)
+        gather(0, 2 * P, T)
+        gather(0, 0, 2 * P)
+        cast_x(1, 1)
+        cast_x(1, 0)
         quantise_x(1, 1)
         gather(1, 3 * P, T)
         quantise_x(1, 0)
         gather(1, 2 * P, 3 * P)
-        gather(1, 0, 2 * P)
+        gather(1, 0, P)
+        gather(1, P, 2 * P)
         sum_a(3, 0)
         sum_a(2, 0)
         sum_a(1, 0)
@@ -239,30 +247,34 @@ def tile_moe_rag_glu_silu_kernel(
         silu(2)
         sum_b(2, 1)
         multiply(2)
+        sum_a(0, 0)
+        sum_b(0, 0)
+        sum_a(0, 1)
+        silu(0)
+        sum_b(0, 1)
         turn(3)
+        multiply(0)
         quantise_h(3)
         sum_a(1, 1)
         silu(1)
         sum_b(1, 1)
-        multiply(1)
-        second_layer(3)
         turn(2)
+        multiply(1)
         quantise_h(2)
-        sum_a(0, 0)
-        sum_a(0, 1)
-        silu(0)
-        sum_b(0, 0)
-        sum_b(0, 1)
-        multiply(0)
+        second_layer(3)
+        turn(0)
+        quantise_h(0)
         second_layer(2)
         turn(1)
         quantise_h(1)
-        turn(0)
-        second_layer(1)
-        quantise_h(0)
         second_layer(0)
-        for lo, hi in ((t * P, (t + 1) * P) for t in ORDER):
+        second_layer(1)
+        for t in ORDER[:-1]:
             for n in range(N_TILES):
-                scatter(lo, hi, n)
+                scatter(out_sb[n], t, n)
         for n in range(N_TILES):
-            nc.sync.dma_start(out[n * P : (n + 1) * P, :], out_sb[n][:])
+            nc.sync.dma_start(out[n * P : (n + 1) * P, HALF:T], out_sb[n][:, HALF:T])
+            nc.scalar.copy(low_sb[n][:], out_sb[n][:, 0:HALF])
+        for n in range(N_TILES):
+            scatter(low_sb[n], ORDER[-1], n)
+            nc.sync.dma_start(out[n * P : (n + 1) * P, 0:HALF], low_sb[n][:])

@@ -26,6 +26,7 @@ FLOPS = 2 * T * (2 * K * H + H * N)
 BYTES = 4 * K * T + 2 * E * (K * H // 2 + K * H // 32) + E * (H * N // 2 + H * N // 32) + 4 * P * T + 2 * P * (T // 16) + 4 * N * T
 
 VECTOR_TOKENS = ((64, 256), (48, 160))
+WORK = (3, 2, 1, 0)
 ORDER = (3, 2, 0, 1)
 
 
@@ -104,11 +105,7 @@ def tile_moe_rag_glu_silu_kernel(
         bank_a = [psum.tile([P, H], F32, name=f"bank_a_{t}") for t in range(TILES)]
         bank_b = [psum.tile([P, H], F32, name=f"bank_b_{t}") for t in range(TILES)]
         acts, hidden, h_grouped, h_codes, grouped = {}, {}, {}, {}, {}
-        y_sb = {(t, n): keep.tile([P, P], F32, name=f"y_{t}_{n}") for n in range(N_TILES) for t in ORDER[-1:]}
-        for t in ORDER[:-1]:
-            y_sb[t] = keep.tile([P, N], F32, name=f"y_{t}")
-            for n in range(N_TILES):
-                y_sb[t, n] = y_sb[t][:, n * P : (n + 1) * P]
+        y_sb = {}
 
         def expert_of(t):
             return 0 if t == 0 else 1
@@ -180,27 +177,33 @@ def tile_moe_rag_glu_silu_kernel(
                 MULT,
             )
 
-        def turn(t):
-            pairs = hidden[t][:].rearrange("p u q d -> p (u q d)").bitcast(F32)
-            for u in range(2):
-                nc.tensor.transpose(bank_a[t][:, u * P : (u + 1) * P], pairs[:, u * P : (u + 1) * P], ident[:])
-            h_grouped[t] = keep.tile([P, P, 4], BF16, name=f"h4_{t}", align_bytes=64)
-            nc.scalar.copy(h_grouped[t][:].bitcast(F32), bank_a[t][:, 0 : 2 * P].rearrange("p (u r) -> p r u", u=2))
-
-        def quantise_h(t):
-            h_words = keep.tile([P, P], U32, name=f"h_words_{t}", align_bytes=64)
-            h_bytes = keep.tile([P, P], U8, name=f"h_bytes_{t}", align_bytes=64)
-            nc.vector.quantize_mx(
-                out=h_words[:].bitcast(FP8X4), scales=h_bytes[:], in_=h_grouped[t][:].rearrange("p r j -> p (r j)")
+        def turn(lo, hi):
+            bank = bank_a[hi - 1]
+            for t in reversed(range(lo, hi)):
+                pairs = hidden[t][:].rearrange("p u q d -> p (u q d)").bitcast(F32)
+                for u in range(2):
+                    at = (2 * (t - lo) + u) * P
+                    nc.tensor.transpose(bank[:, at : at + P], pairs[:, u * P : (u + 1) * P], ident[:])
+            h_grouped[lo] = keep.tile([P, (hi - lo) * P, 4], BF16, name=f"h4_{lo}", align_bytes=64)
+            nc.scalar.copy(
+                h_grouped[lo][:].bitcast(F32).rearrange("p (t r) u -> p t r u", r=P),
+                bank[:, 0 : 2 * (hi - lo) * P].rearrange("p (t u r) -> p t r u", u=2, r=P),
             )
-            h_codes[t] = (h_words, h_bytes)
 
-        def second_layer(t):
-            e = expert_of(t)
-            h_words, h_bytes = h_codes[t]
+        def quantise_h(lo, hi):
+            h_words = keep.tile([P, (hi - lo) * P], U32, name=f"h_words_{lo}", align_bytes=64)
+            h_bytes = keep.tile([P, (hi - lo) * P], U8, name=f"h_bytes_{lo}", align_bytes=64)
+            nc.vector.quantize_mx(
+                out=h_words[:].bitcast(FP8X4), scales=h_bytes[:], in_=h_grouped[lo][:].rearrange("p r j -> p (r j)")
+            )
+            h_codes[lo] = (h_words, h_bytes)
+
+        def second_layer(lo, hi, sums):
+            e = expert_of(lo)
+            h_words, h_bytes = h_codes[lo]
             for n in range(N_TILES):
                 nc.tensor.matmul_mx(
-                    out=bank_b[t][:, n * P : (n + 1) * P],
+                    out=sums[n],
                     lhsT=w2[:, e, 2 * P * n : 2 * P * (n + 1)].bitcast(FP4X4),
                     lhsT_scale=w2_sc[:, e, P * n : P * (n + 1)],
                     rhs=h_words[:].bitcast(FP8X4),
@@ -208,16 +211,41 @@ def tile_moe_rag_glu_silu_kernel(
                     start=True,
                     stop=True,
                 )
-            if t == ORDER[-1]:
-                for n in range(N_TILES):
-                    nc.scalar.copy(y_sb[t, n][:], bank_b[t][:, n * P : (n + 1) * P])
-            else:
-                nc.scalar.copy(y_sb[t][:], bank_b[t][:, 0:N])
 
-        def scatter(window, t, n):
-            lo, hi = t * P, (t + 1) * P
+        def second_layer_pair():
+            sums = [bank_b[3][:, 0:HALF], bank_b[2][:, 0:HALF], bank_a[2][:, 0:HALF]]
+            second_layer(2, 4, sums)
+            for n in range(N_TILES):
+                y_sb[2, n] = keep.tile([P, HALF], F32, name=f"y_2_{n}")
+                nc.scalar.copy(y_sb[2, n][:], sums[n])
+
+        def second_layer_single(t, bank):
+            second_layer(t, t + 1, [bank[:, n * P : (n + 1) * P] for n in range(N_TILES)])
+            y = keep.tile([P, N], F32, name=f"y_{t}")
+            nc.scalar.copy(y[:], bank[:, 0:N])
+            for n in range(N_TILES):
+                y_sb[t, n] = y[:, n * P : (n + 1) * P]
+
+        def scatter(window, t, t_end, n):
+            lo, hi = t * P, t_end * P
             where = offsets[:, lo // 16 : hi // 16]
             nc.vector.tensor_tensor(window[:].indirect(where), y_sb[t, n][:], gate_sb[:, lo:hi], MULT)
+
+        blank = keep.tile([P, 4 * P], BF16, name="blank", align_bytes=64)
+        blank_words = keep.tile([P, P], U32, name="blank_words", align_bytes=64)
+        blank_bytes = keep.tile([P, P], U8, name="blank_bytes", align_bytes=64)
+        nc.vector.memset(blank[:], 1.0)
+        nc.vector.quantize_mx(out=blank_words[:].bitcast(FP8X4), scales=blank_bytes[:], in_=blank[:])
+        for again in range(3):
+            nc.tensor.matmul_mx(
+                out=bank_b[0][:],
+                lhsT=blank_words[:].bitcast(FP8X4),
+                lhsT_scale=blank_bytes[:],
+                rhs=w1[1, 0].bitcast(FP4X4),
+                rhs_scale=w1_sc[:, PASSES, :],
+                start=True,
+                stop=True,
+            )
 
         cast_x(0, 1)
         cast_x(0, 0)
@@ -231,8 +259,8 @@ def tile_moe_rag_glu_silu_kernel(
         gather(1, 3 * P, T)
         quantise_x(1, 0)
         gather(1, 2 * P, 3 * P)
-        gather(1, 0, P)
         gather(1, P, 2 * P)
+        gather(1, 0, P)
         sum_a(3, 0)
         sum_a(2, 0)
         sum_a(1, 0)
@@ -247,34 +275,28 @@ def tile_moe_rag_glu_silu_kernel(
         silu(2)
         sum_b(2, 1)
         multiply(2)
-        sum_a(0, 0)
-        sum_b(0, 0)
-        sum_a(0, 1)
-        silu(0)
-        sum_b(0, 1)
-        turn(3)
-        multiply(0)
-        quantise_h(3)
         sum_a(1, 1)
         silu(1)
         sum_b(1, 1)
-        turn(2)
         multiply(1)
-        quantise_h(2)
-        second_layer(3)
-        turn(0)
-        quantise_h(0)
-        second_layer(2)
-        turn(1)
-        quantise_h(1)
-        second_layer(0)
-        second_layer(1)
-        for t in ORDER[:-1]:
+        sum_a(0, 0)
+        sum_a(0, 1)
+        silu(0)
+        sum_b(0, 0)
+        sum_b(0, 1)
+        multiply(0)
+        for lo, hi in ((2, 4), (1, 2), (0, 1)):
+            turn(lo, hi)
+            quantise_h(lo, hi)
+        second_layer_pair()
+        second_layer_single(0, bank_b[0])
+        second_layer_single(1, bank_b[2])
+        for lo, hi in ((2, 4), (0, 1)):
             for n in range(N_TILES):
-                scatter(out_sb[n], t, n)
+                scatter(out_sb[n], lo, hi, n)
         for n in range(N_TILES):
             nc.sync.dma_start(out[n * P : (n + 1) * P, HALF:T], out_sb[n][:, HALF:T])
             nc.scalar.copy(low_sb[n][:], out_sb[n][:, 0:HALF])
         for n in range(N_TILES):
-            scatter(low_sb[n], ORDER[-1], n)
+            scatter(low_sb[n], 1, 2, n)
             nc.sync.dma_start(out[n * P : (n + 1) * P, 0:HALF], low_sb[n][:])

@@ -61,10 +61,6 @@ def tile_moe_rag_glu_silu_kernel(
             for s in range(lo, hi):
                 held[e, s] = codes[:, s - lo, :]
 
-        warm = keep.tile([P, 2], F32, name="warm")
-        nc.vector.memset(warm[:, 0:1], 0.0)
-        nc.scalar.activation(warm[:, 1:2], warm[:, 0:1], ACT.Silu)
-
         w1_sc = scale_plane("w1", w1_scales)
         w3_sc = scale_plane("w3", w3_scales)
         w2_sc = scale_plane("w2", w2_scales)
@@ -230,22 +226,6 @@ def tile_moe_rag_glu_silu_kernel(
             lo, hi = t * P, t_end * P
             where = offsets[:, lo // 16 : hi // 16]
             nc.vector.tensor_tensor(window[:].indirect(where), y_sb[t, n][:], gate_sb[:, lo:hi], MULT)
-
-        blank = keep.tile([P, 4 * P], BF16, name="blank", align_bytes=64)
-        blank_words = keep.tile([P, P], U32, name="blank_words", align_bytes=64)
-        blank_bytes = keep.tile([P, P], U8, name="blank_bytes", align_bytes=64)
-        nc.vector.memset(blank[:], 1.0)
-        nc.vector.quantize_mx(out=blank_words[:].bitcast(FP8X4), scales=blank_bytes[:], in_=blank[:])
-        for again in range(3):
-            nc.tensor.matmul_mx(
-                out=bank_b[0][:],
-                lhsT=blank_words[:].bitcast(FP8X4),
-                lhsT_scale=blank_bytes[:],
-                rhs=w1[1, 0].bitcast(FP4X4),
-                rhs_scale=w1_sc[:, PASSES, :],
-                start=True,
-                stop=True,
-            )
 
         cast_x(0, 1)
         cast_x(0, 0)

@@ -19,15 +19,15 @@ MULT = mybir.AluOpType.mult
 P = 128
 PASSES = K // 512
 HALF = T // 2
+LOW, HIGH = 0, 1
 TILES = T // P
-N_TILES = N // P
+BLOCKS = N // P
+OFFSETS_A_COLUMN = 16
 
 FLOPS = 2 * T * (2 * K * H + H * N)
 BYTES = 4 * K * T + 2 * E * (K * H // 2 + K * H // 32) + E * (H * N // 2 + H * N // 32) + 4 * P * T + 2 * P * (T // 16) + 4 * N * T
 
 VECTOR_TOKENS = ((64, 256), (48, 160))
-WORK = (3, 2, 1, 0)
-ORDER = (3, 2, 0, 1)
 
 
 def tile_moe_rag_glu_silu_kernel(
@@ -36,18 +36,17 @@ def tile_moe_rag_glu_silu_kernel(
     nc = tc.nc
     with ExitStack() as ctx:
         keep = ctx.enter_context(tc.tile_pool(name="keep", bufs=1))
-        reuse = ctx.enter_context(tc.tile_pool(name="reuse", bufs=1))
         psum = ctx.enter_context(tc.psum_pool(name="psum", bufs=1))
 
-        def scale_plane(name, scales):
-            plane = keep.tile([P, E * scales.shape[1], scales.shape[3]], U8, name=f"{name}_plane", align_bytes=64)
-            nc.vector.memset(plane[:].bitcast(I32), 0)
-            return plane
+        def scale_tile(name, scales):
+            tile = keep.tile([P, E * scales.shape[1], scales.shape[3]], U8, name=f"{name}_scales", align_bytes=64)
+            nc.vector.memset(tile[:].bitcast(I32), 0)
+            return tile
 
-        def load_scales(plane, scales):
+        def load_scales(tile, scales):
             rows = scales.bitcast(I32).rearrange("e s (g r) i -> r g (e s) i", r=4)
             for r in range(4):
-                nc.sync.dma_start(plane[r:P:32, :, :].bitcast(I32), rows[r])
+                nc.sync.dma_start(tile[r:P:32, :, :].bitcast(I32), rows[r])
 
         def load_x(s):
             rows = xT[s * 512 : (s + 1) * 512, :].rearrange("(p j) w -> p j w", j=4)
@@ -55,35 +54,35 @@ def tile_moe_rag_glu_silu_kernel(
             nc.sync.dma_start(raw[:], rows)
             return raw
 
-        def load_words(name, held, words, e, lo, hi):
-            codes = keep.tile([P, hi - lo, words.shape[3]], U8, name=f"{name}_codes_{e}_{lo}", align_bytes=64)
-            nc.sync.dma_start(codes[:].bitcast(I32), words.bitcast(I32)[e, lo:hi].rearrange("s p b -> p s b"))
-            for s in range(lo, hi):
-                held[e, s] = codes[:, s - lo, :]
+        def load_words(name, held, words, e, first_pass, end_pass):
+            codes = keep.tile([P, end_pass - first_pass, words.shape[3]], U8, name=f"{name}_codes_{e}_{first_pass}", align_bytes=64)
+            nc.sync.dma_start(codes[:].bitcast(I32), words.bitcast(I32)[e, first_pass:end_pass].rearrange("s p b -> p s b"))
+            for s in range(first_pass, end_pass):
+                held[e, s] = codes[:, s - first_pass, :]
 
-        w1_sc = scale_plane("w1", w1_scales)
-        w3_sc = scale_plane("w3", w3_scales)
-        w2_sc = scale_plane("w2", w2_scales)
+        w1_sc = scale_tile("w1", w1_scales)
+        w3_sc = scale_tile("w3", w3_scales)
+        w2_sc = scale_tile("w2", w2_scales)
         all_words, all_bytes, slot_words, slot_bytes = [], [], {}, {}
         for s in range(PASSES):
             all_words.append(keep.tile([P, T], I32, name=f"all_words_{s}", align_bytes=64))
             all_bytes.append(keep.tile([P, T], U8, name=f"all_bytes_{s}", align_bytes=64))
             nc.vector.memset(all_bytes[s][:].bitcast(I32), 0)
-
         nc.vector.memset(all_words[1][:, 0:HALF], 0)
 
-        offsets = keep.tile([P, T // 16], U16, name="offsets")
+        offsets = keep.tile([P, T // OFFSETS_A_COLUMN], U16, name="offsets")
         x_raw, w1, w3 = {}, {}, {}
         x_raw[0] = load_x(0)
         nc.sync.dma_start(offsets[:], offs)
         load_scales(w1_sc, w1_scales)
         load_words("w1", w1, w1_words, 1, 0, 1)
         x_raw[1] = load_x(1)
+        load_words("w1", w1, w1_words, 0, 0, 1)
         load_scales(w3_sc, w3_scales)
         load_words("w3", w3, w3_words, 1, 0, 1)
         load_words("w1", w1, w1_words, 1, 1, 2)
         load_words("w3", w3, w3_words, 1, 1, 2)
-        load_words("w1", w1, w1_words, 0, 0, 2)
+        load_words("w1", w1, w1_words, 0, 1, 2)
         load_words("w3", w3, w3_words, 0, 0, 2)
         load_scales(w2_sc, w2_scales)
         w2 = keep.tile([P, E, 2 * N], U8, name="w2", align_bytes=64)
@@ -94,24 +93,27 @@ def tile_moe_rag_glu_silu_kernel(
         ident = keep.tile([P, P], F32, name="ident")
         make_identity(nc, ident[:])
 
-        out_sb = [keep.tile([P, T], F32, name=f"out_sb_{n}") for n in range(N_TILES)]
-        low_sb = [keep.tile([P, HALF], F32, name=f"low_sb_{n}") for n in range(N_TILES)]
-        for n in range(N_TILES):
+        out_sb = [keep.tile([P, T], F32, name=f"out_sb_{n}") for n in range(BLOCKS)]
+        low_sb = [keep.tile([P, HALF], F32, name=f"low_sb_{n}") for n in range(BLOCKS)]
+        for n in range(BLOCKS):
             nc.vector.memset(out_sb[n][:, 0:HALF], 0.0)
         bank_a = [psum.tile([P, H], F32, name=f"bank_a_{t}") for t in range(TILES)]
         bank_b = [psum.tile([P, H], F32, name=f"bank_b_{t}") for t in range(TILES)]
-        acts, hidden, h_grouped, h_codes, grouped = {}, {}, {}, {}, {}
-        y_sb = {}
+        x_grouped, silu_a, hidden, h_grouped, h_codes, y_sb = {}, {}, {}, {}, {}, {}
 
         def expert_of(t):
             return 0 if t == 0 else 1
 
+        def offsets_of(first_tile, end_tile):
+            return offsets[:, first_tile * P // OFFSETS_A_COLUMN : end_tile * P // OFFSETS_A_COLUMN]
+
         def cast_x(s, half):
-            grouped[s, half] = keep.tile([P, HALF, 4], BF16, name=f"grouped_{s}_{half}", align_bytes=64)
-            for copy, lo, hi in ((nc.scalar.copy, VECTOR_TOKENS[s][half], HALF), (nc.vector.tensor_copy, 0, VECTOR_TOKENS[s][half])):
+            x_grouped[s, half] = keep.tile([P, HALF, 4], BF16, name=f"x_grouped_{s}_{half}", align_bytes=64)
+            share = VECTOR_TOKENS[s][half]
+            for copy, lo, hi in ((nc.scalar.copy, share, HALF), (nc.vector.tensor_copy, 0, share)):
                 if hi > lo:
                     copy(
-                        grouped[s, half][:, lo:hi, :].rearrange("p (c i) j -> p c j i", i=4),
+                        x_grouped[s, half][:, lo:hi, :].rearrange("p (c i) j -> p c j i", i=4),
                         x_raw[s][:, :, half * HALF + lo : half * HALF + hi].rearrange("p j (c i) -> p c j i", i=4),
                     )
 
@@ -120,36 +122,28 @@ def tile_moe_rag_glu_silu_kernel(
             nc.vector.quantize_mx(
                 out=all_words[s][:, cols].bitcast(FP8X4),
                 scales=all_bytes[s][:, cols],
-                in_=grouped[s, half][:].rearrange("p w j -> p (w j)"),
+                in_=x_grouped[s, half][:].rearrange("p w j -> p (w j)"),
             )
 
-        def gather_words(s, lo, hi, over=False):
-            if over:
-                words = reuse.tile([P, hi - lo], U32, name=f"slot_words_{s}_{lo}", align_bytes=64, offset=0)
-            else:
-                words = keep.tile([P, hi - lo], U32, name=f"slot_words_{s}_{lo}", align_bytes=64)
-            nc.vector.tensor_copy(words[:], all_words[s][:].bitcast(U32).indirect(offsets[:, lo // 16 : hi // 16]))
-            for t in range(lo // P, hi // P):
-                slot_words[s, t] = words[:, t * P - lo : (t + 1) * P - lo]
+        def gather(s, first_tile, end_tile):
+            slots = (end_tile - first_tile) * P
+            words = keep.tile([P, slots], U32, name=f"slot_words_{s}_{first_tile}", align_bytes=64)
+            nc.vector.tensor_copy(words[:], all_words[s][:].bitcast(U32).indirect(offsets_of(first_tile, end_tile)))
+            scale_bytes = keep.tile([P, slots], U8, name=f"slot_bytes_{s}_{first_tile}", align_bytes=64)
+            nc.vector.tensor_copy(scale_bytes[:], all_bytes[s][:].indirect(offsets_of(first_tile, end_tile)))
+            for t in range(first_tile, end_tile):
+                cols = slice((t - first_tile) * P, (t - first_tile + 1) * P)
+                slot_words[s, t] = words[:, cols]
+                slot_bytes[s, t] = scale_bytes[:, cols]
 
-        def gather_bytes(s, lo, hi):
-            scale_bytes = keep.tile([P, hi - lo], U8, name=f"slot_bytes_{s}_{lo}", align_bytes=64)
-            nc.vector.tensor_copy(scale_bytes[:], all_bytes[s][:].indirect(offsets[:, lo // 16 : hi // 16]))
-            for t in range(lo // P, hi // P):
-                slot_bytes[s, t] = scale_bytes[:, t * P - lo : (t + 1) * P - lo]
-
-        def gather(s, lo, hi, over=False):
-            gather_words(s, lo, hi, over)
-            gather_bytes(s, lo, hi)
-
-        def first_layer(t, s, bank, codes, plane):
+        def first_layer(t, s, bank, codes, scales):
             e = expert_of(t)
             nc.tensor.matmul_mx(
                 out=bank[t][:],
                 lhsT=slot_words[s, t].bitcast(FP8X4),
                 lhsT_scale=slot_bytes[s, t],
                 rhs=codes[e, s].bitcast(FP4X4),
-                rhs_scale=plane[:, PASSES * e + s, :],
+                rhs_scale=scales[:, PASSES * e + s, :],
                 start=(s == 0),
                 stop=(s == PASSES - 1),
             )
@@ -161,43 +155,52 @@ def tile_moe_rag_glu_silu_kernel(
             first_layer(t, s, bank_b, w3, w3_sc)
 
         def silu(t):
-            acts[t] = keep.tile([P, H], F32, name=f"act_{t}")
-            nc.scalar.activation(acts[t][:], bank_a[t][:], ACT.Silu)
+            silu_a[t] = keep.tile([P, H], F32, name=f"silu_a_{t}")
+            nc.scalar.activation(silu_a[t][:], bank_a[t][:], ACT.Silu)
 
         def multiply(t):
             hidden[t] = keep.tile([P, 2, P, 2], BF16, name=f"h_{t}", align_bytes=64)
             nc.vector.tensor_tensor(
                 hidden[t][:],
-                acts[t][:].rearrange("p (q u d) -> p u q d", u=2, d=2),
+                silu_a[t][:].rearrange("p (q u d) -> p u q d", u=2, d=2),
                 bank_b[t][:].rearrange("p (q u d) -> p u q d", u=2, d=2),
                 MULT,
             )
 
-        def turn(lo, hi):
-            bank = bank_a[hi - 1]
-            for t in reversed(range(lo, hi)):
+        def finish_tile(t, b_passes):
+            sum_a(t, 1)
+            silu(t)
+            for s in b_passes:
+                sum_b(t, s)
+            multiply(t)
+
+        def turn(first_tile, end_tile):
+            tiles = end_tile - first_tile
+            bank = bank_a[end_tile - 1]
+            for t in reversed(range(first_tile, end_tile)):
                 pairs = hidden[t][:].rearrange("p u q d -> p (u q d)").bitcast(F32)
                 for u in range(2):
-                    at = (2 * (t - lo) + u) * P
+                    at = (2 * (t - first_tile) + u) * P
                     nc.tensor.transpose(bank[:, at : at + P], pairs[:, u * P : (u + 1) * P], ident[:])
-            h_grouped[lo] = keep.tile([P, (hi - lo) * P, 4], BF16, name=f"h4_{lo}", align_bytes=64)
+            h_grouped[first_tile] = keep.tile([P, tiles * P, 4], BF16, name=f"h_grouped_{first_tile}", align_bytes=64)
             nc.scalar.copy(
-                h_grouped[lo][:].bitcast(F32).rearrange("p (t r) u -> p t r u", r=P),
-                bank[:, 0 : 2 * (hi - lo) * P].rearrange("p (t u r) -> p t r u", u=2, r=P),
+                h_grouped[first_tile][:].bitcast(F32).rearrange("p (t r) u -> p t r u", r=P),
+                bank[:, 0 : 2 * tiles * P].rearrange("p (t u r) -> p t r u", u=2, r=P),
             )
 
-        def quantise_h(lo, hi):
-            h_words = keep.tile([P, (hi - lo) * P], U32, name=f"h_words_{lo}", align_bytes=64)
-            h_bytes = keep.tile([P, (hi - lo) * P], U8, name=f"h_bytes_{lo}", align_bytes=64)
+        def quantise_h(first_tile, end_tile):
+            slots = (end_tile - first_tile) * P
+            h_words = keep.tile([P, slots], U32, name=f"h_words_{first_tile}", align_bytes=64)
+            h_bytes = keep.tile([P, slots], U8, name=f"h_bytes_{first_tile}", align_bytes=64)
             nc.vector.quantize_mx(
-                out=h_words[:].bitcast(FP8X4), scales=h_bytes[:], in_=h_grouped[lo][:].rearrange("p r j -> p (r j)")
+                out=h_words[:].bitcast(FP8X4), scales=h_bytes[:], in_=h_grouped[first_tile][:].rearrange("p r j -> p (r j)")
             )
-            h_codes[lo] = (h_words, h_bytes)
+            h_codes[first_tile] = (h_words, h_bytes)
 
-        def second_layer(lo, hi, sums):
-            e = expert_of(lo)
-            h_words, h_bytes = h_codes[lo]
-            for n in range(N_TILES):
+        def second_layer(first_tile, sums):
+            e = expert_of(first_tile)
+            h_words, h_bytes = h_codes[first_tile]
+            for n in range(BLOCKS):
                 nc.tensor.matmul_mx(
                     out=sums[n],
                     lhsT=w2[:, e, 2 * P * n : 2 * P * (n + 1)].bitcast(FP4X4),
@@ -208,75 +211,67 @@ def tile_moe_rag_glu_silu_kernel(
                     stop=True,
                 )
 
-        def second_layer_pair():
-            sums = [bank_b[3][:, 0:HALF], bank_b[2][:, 0:HALF], bank_a[2][:, 0:HALF]]
-            second_layer(2, 4, sums)
-            for n in range(N_TILES):
-                y_sb[2, n] = keep.tile([P, HALF], F32, name=f"y_2_{n}")
-                nc.scalar.copy(y_sb[2, n][:], sums[n])
+        def second_layer_of_tiles_2_and_3():
+            sums = [bank[:, 0 : 2 * P] for bank in (bank_b[3], bank_b[2], bank_a[2])]
+            second_layer(2, sums)
+            for n in range(BLOCKS):
+                y = keep.tile([P, 2 * P], F32, name=f"y_2_{n}")
+                nc.scalar.copy(y[:], sums[n])
+                y_sb[2, n] = y[:]
 
-        def second_layer_single(t, bank):
-            second_layer(t, t + 1, [bank[:, n * P : (n + 1) * P] for n in range(N_TILES)])
+        def second_layer_of_tile(t, bank):
+            second_layer(t, [bank[:, n * P : (n + 1) * P] for n in range(BLOCKS)])
             y = keep.tile([P, N], F32, name=f"y_{t}")
             nc.scalar.copy(y[:], bank[:, 0:N])
-            for n in range(N_TILES):
+            for n in range(BLOCKS):
                 y_sb[t, n] = y[:, n * P : (n + 1) * P]
 
-        def scatter(window, t, t_end, n):
-            lo, hi = t * P, t_end * P
-            where = offsets[:, lo // 16 : hi // 16]
-            nc.vector.tensor_tensor(window[:].indirect(where), y_sb[t, n][:], gate_sb[:, lo:hi], MULT)
+        def scatter(window, first_tile, end_tile, n):
+            nc.vector.tensor_tensor(
+                window[:].indirect(offsets_of(first_tile, end_tile)),
+                y_sb[first_tile, n],
+                gate_sb[:, first_tile * P : end_tile * P],
+                MULT,
+            )
 
-        cast_x(0, 1)
-        cast_x(0, 0)
-        quantise_x(0, 1)
-        quantise_x(0, 0)
-        gather(0, 2 * P, T)
-        gather(0, 0, 2 * P)
-        cast_x(1, 1)
-        cast_x(1, 0)
-        quantise_x(1, 1)
-        gather(1, 3 * P, T)
-        quantise_x(1, 0)
-        gather(1, 2 * P, 3 * P)
-        gather(1, P, 2 * P)
-        gather(1, 0, P)
-        sum_a(3, 0)
-        sum_a(2, 0)
-        sum_a(1, 0)
+        cast_x(0, HIGH)
+        cast_x(0, LOW)
+        quantise_x(0, HIGH)
+        quantise_x(0, LOW)
+        gather(0, 3, 4)
+        gather(0, 2, 3)
+        gather(0, 0, 2)
+        cast_x(1, HIGH)
+        cast_x(1, LOW)
+        quantise_x(1, HIGH)
+        gather(1, 3, 4)
+        quantise_x(1, LOW)
+        for t in (2, 1, 0):
+            gather(1, t, t + 1)
+
+        for t in (3, 2, 1, 0):
+            sum_a(t, 0)
         sum_b(3, 0)
-        sum_a(3, 1)
-        silu(3)
-        sum_b(3, 1)
-        multiply(3)
+        finish_tile(3, (1,))
         sum_b(2, 0)
         sum_b(1, 0)
-        sum_a(2, 1)
-        silu(2)
-        sum_b(2, 1)
-        multiply(2)
-        sum_a(1, 1)
-        silu(1)
-        sum_b(1, 1)
-        multiply(1)
-        sum_a(0, 0)
-        sum_a(0, 1)
-        silu(0)
-        sum_b(0, 0)
-        sum_b(0, 1)
-        multiply(0)
-        for lo, hi in ((2, 4), (1, 2), (0, 1)):
-            turn(lo, hi)
-            quantise_h(lo, hi)
-        second_layer_pair()
-        second_layer_single(0, bank_b[0])
-        second_layer_single(1, bank_b[2])
-        for lo, hi in ((2, 4), (0, 1)):
-            for n in range(N_TILES):
-                scatter(out_sb[n], lo, hi, n)
-        for n in range(N_TILES):
+        finish_tile(2, (1,))
+        finish_tile(1, (1,))
+        finish_tile(0, (0, 1))
+
+        for first_tile, end_tile in ((2, 4), (1, 2), (0, 1)):
+            turn(first_tile, end_tile)
+            quantise_h(first_tile, end_tile)
+        second_layer_of_tiles_2_and_3()
+        second_layer_of_tile(0, bank_b[0])
+        second_layer_of_tile(1, bank_b[2])
+
+        for first_tile, end_tile in ((2, 4), (0, 1)):
+            for n in range(BLOCKS):
+                scatter(out_sb[n], first_tile, end_tile, n)
+        for n in range(BLOCKS):
             nc.sync.dma_start(out[n * P : (n + 1) * P, HALF:T], out_sb[n][:, HALF:T])
             nc.scalar.copy(low_sb[n][:], out_sb[n][:, 0:HALF])
-        for n in range(N_TILES):
+        for n in range(BLOCKS):
             scatter(low_sb[n], 1, 2, n)
             nc.sync.dma_start(out[n * P : (n + 1) * P, 0:HALF], low_sb[n][:])

@@ -20,6 +20,7 @@ P = 128
 PASSES = K // 512
 HALF = T // 2
 LOW, HIGH = 0, 1
+FIRST, SECOND = 1, 0
 TILES = T // P
 BLOCKS = N // P
 OFFSETS_A_COLUMN = 16
@@ -27,7 +28,7 @@ OFFSETS_A_COLUMN = 16
 FLOPS = 2 * T * (2 * K * H + H * N)
 BYTES = 4 * K * T + 2 * E * (K * H // 2 + K * H // 32) + E * (H * N // 2 + H * N // 32) + 4 * P * T + 2 * P * (T // 16) + 4 * N * T
 
-VECTOR_TOKENS = ((64, 256), (48, 160))
+VECTOR_TOKENS = {FIRST: (64, 256), SECOND: (48, 160)}
 
 
 def tile_moe_rag_glu_silu_kernel(
@@ -38,15 +39,15 @@ def tile_moe_rag_glu_silu_kernel(
         keep = ctx.enter_context(tc.tile_pool(name="keep", bufs=1))
         psum = ctx.enter_context(tc.psum_pool(name="psum", bufs=1))
 
-        def scale_tile(name, scales):
-            tile = keep.tile([P, E * scales.shape[1], scales.shape[3]], U8, name=f"{name}_scales", align_bytes=64)
+        def scale_tile(name, scales, first, end):
+            tile = keep.tile([P, end - first, scales.shape[3]], U8, name=f"{name}_scales_{first}", align_bytes=64)
             nc.vector.memset(tile[:].bitcast(I32), 0)
             return tile
 
-        def load_scales(tile, scales):
+        def load_scales(tile, scales, first, end):
             rows = scales.bitcast(I32).rearrange("e s (g r) i -> r g (e s) i", r=4)
             for r in range(4):
-                nc.sync.dma_start(tile[r:P:32, :, :].bitcast(I32), rows[r])
+                nc.sync.dma_start(tile[r:P:32, :, :].bitcast(I32), rows[r][:, first:end, :])
 
         def load_x(s):
             rows = xT[s * 512 : (s + 1) * 512, :].rearrange("(p j) w -> p j w", j=4)
@@ -60,31 +61,35 @@ def tile_moe_rag_glu_silu_kernel(
             for s in range(first_pass, end_pass):
                 held[e, s] = codes[:, s - first_pass, :]
 
-        w1_sc = scale_tile("w1", w1_scales)
-        w3_sc = scale_tile("w3", w3_scales)
-        w2_sc = scale_tile("w2", w2_scales)
+        w1_early = scale_tile("w1", w1_scales, 3, 4)
+        w1_rest = scale_tile("w1", w1_scales, 0, 3)
+        w3_all = scale_tile("w3", w3_scales, 0, 4)
+        w2_sc = scale_tile("w2", w2_scales, 0, 2)
+        w1_sc = [w1_rest[:, 0, :], w1_rest[:, 1, :], w1_rest[:, 2, :], w1_early[:, 0, :]]
+        w3_sc = [w3_all[:, plane, :] for plane in range(E * PASSES)]
         all_words, all_bytes, slot_words, slot_bytes = [], [], {}, {}
         for s in range(PASSES):
             all_words.append(keep.tile([P, T], I32, name=f"all_words_{s}", align_bytes=64))
             all_bytes.append(keep.tile([P, T], U8, name=f"all_bytes_{s}", align_bytes=64))
             nc.vector.memset(all_bytes[s][:].bitcast(I32), 0)
-        nc.vector.memset(all_words[1][:, 0:HALF], 0)
+        nc.vector.memset(all_words[SECOND][:, 0:HALF], 0)
 
         offsets = keep.tile([P, T // OFFSETS_A_COLUMN], U16, name="offsets")
         x_raw, w1, w3 = {}, {}, {}
-        x_raw[0] = load_x(0)
+        x_raw[FIRST] = load_x(FIRST)
         nc.sync.dma_start(offsets[:], offs)
-        load_scales(w1_sc, w1_scales)
-        load_words("w1", w1, w1_words, 1, 0, 1)
-        x_raw[1] = load_x(1)
-        load_words("w1", w1, w1_words, 0, 0, 1)
-        load_scales(w3_sc, w3_scales)
-        load_words("w3", w3, w3_words, 1, 0, 1)
-        load_words("w1", w1, w1_words, 1, 1, 2)
-        load_words("w3", w3, w3_words, 1, 1, 2)
-        load_words("w1", w1, w1_words, 0, 1, 2)
+        load_scales(w1_early, w1_scales, 3, 4)
+        load_words("w1", w1, w1_words, 1, FIRST, FIRST + 1)
+        x_raw[SECOND] = load_x(SECOND)
+        load_scales(w1_rest, w1_scales, 0, 3)
+        load_words("w1", w1, w1_words, 0, FIRST, FIRST + 1)
+        load_scales(w3_all, w3_scales, 0, 4)
+        load_words("w3", w3, w3_words, 1, FIRST, FIRST + 1)
+        load_words("w1", w1, w1_words, 1, SECOND, SECOND + 1)
+        load_words("w3", w3, w3_words, 1, SECOND, SECOND + 1)
+        load_words("w1", w1, w1_words, 0, SECOND, SECOND + 1)
         load_words("w3", w3, w3_words, 0, 0, 2)
-        load_scales(w2_sc, w2_scales)
+        load_scales(w2_sc, w2_scales, 0, 2)
         w2 = keep.tile([P, E, 2 * N], U8, name="w2", align_bytes=64)
         nc.sync.dma_start(w2[:].bitcast(I32), w2_words.bitcast(I32)[:, 0].rearrange("e p b -> p e b"))
         gate_sb = keep.tile([P, T], F32, name="gate_sb")
@@ -95,8 +100,9 @@ def tile_moe_rag_glu_silu_kernel(
 
         out_sb = [keep.tile([P, T], F32, name=f"out_sb_{n}") for n in range(BLOCKS)]
         low_sb = [keep.tile([P, HALF], F32, name=f"low_sb_{n}") for n in range(BLOCKS)]
-        for n in range(BLOCKS):
-            nc.vector.memset(out_sb[n][:, 0:HALF], 0.0)
+        nc.vector.memset(out_sb[0][:, 0:HALF], 0.0)
+        for n in range(1, BLOCKS):
+            nc.scalar.activation(out_sb[n][:, 0:HALF], out_sb[0][:, 0:HALF], ACT.Silu)
         bank_a = [psum.tile([P, H], F32, name=f"bank_a_{t}") for t in range(TILES)]
         bank_b = [psum.tile([P, H], F32, name=f"bank_b_{t}") for t in range(TILES)]
         x_grouped, silu_a, hidden, h_grouped, h_codes, y_sb = {}, {}, {}, {}, {}, {}
@@ -143,9 +149,9 @@ def tile_moe_rag_glu_silu_kernel(
                 lhsT=slot_words[s, t].bitcast(FP8X4),
                 lhsT_scale=slot_bytes[s, t],
                 rhs=codes[e, s].bitcast(FP4X4),
-                rhs_scale=scales[:, PASSES * e + s, :],
-                start=(s == 0),
-                stop=(s == PASSES - 1),
+                rhs_scale=scales[PASSES * e + s],
+                start=(s == FIRST),
+                stop=(s == SECOND),
             )
 
         def sum_a(t, s):
@@ -168,25 +174,22 @@ def tile_moe_rag_glu_silu_kernel(
             )
 
         def finish_tile(t, b_passes):
-            sum_a(t, 1)
+            sum_a(t, SECOND)
             silu(t)
             for s in b_passes:
                 sum_b(t, s)
             multiply(t)
 
         def turn(first_tile, end_tile):
-            tiles = end_tile - first_tile
-            bank = bank_a[end_tile - 1]
+            h_grouped[first_tile] = keep.tile([P, (end_tile - first_tile) * P, 4], BF16, name=f"h_grouped_{first_tile}", align_bytes=64)
             for t in reversed(range(first_tile, end_tile)):
                 pairs = hidden[t][:].rearrange("p u q d -> p (u q d)").bitcast(F32)
                 for u in range(2):
-                    at = (2 * (t - first_tile) + u) * P
-                    nc.tensor.transpose(bank[:, at : at + P], pairs[:, u * P : (u + 1) * P], ident[:])
-            h_grouped[first_tile] = keep.tile([P, tiles * P, 4], BF16, name=f"h_grouped_{first_tile}", align_bytes=64)
-            nc.scalar.copy(
-                h_grouped[first_tile][:].bitcast(F32).rearrange("p (t r) u -> p t r u", r=P),
-                bank[:, 0 : 2 * tiles * P].rearrange("p (t u r) -> p t r u", u=2, r=P),
-            )
+                    nc.tensor.transpose(bank_a[t][:, u * P : (u + 1) * P], pairs[:, u * P : (u + 1) * P], ident[:])
+                nc.scalar.copy(
+                    h_grouped[first_tile][:, (t - first_tile) * P : (t - first_tile + 1) * P, :].bitcast(F32),
+                    bank_a[t][:, 0 : 2 * P].rearrange("p (u r) -> p r u", u=2),
+                )
 
         def quantise_h(first_tile, end_tile):
             slots = (end_tile - first_tile) * P
@@ -212,7 +215,7 @@ def tile_moe_rag_glu_silu_kernel(
                 )
 
         def second_layer_of_tiles_2_and_3():
-            sums = [bank[:, 0 : 2 * P] for bank in (bank_b[3], bank_b[2], bank_a[2])]
+            sums = [bank[:, 0 : 2 * P] for bank in (bank_b[3], bank_b[2], bank_a[3])]
             second_layer(2, sums)
             for n in range(BLOCKS):
                 y = keep.tile([P, 2 * P], F32, name=f"y_2_{n}")
@@ -234,30 +237,30 @@ def tile_moe_rag_glu_silu_kernel(
                 MULT,
             )
 
-        cast_x(0, HIGH)
-        cast_x(0, LOW)
-        quantise_x(0, HIGH)
-        quantise_x(0, LOW)
-        gather(0, 3, 4)
-        gather(0, 2, 3)
-        gather(0, 0, 2)
-        cast_x(1, HIGH)
-        cast_x(1, LOW)
-        quantise_x(1, HIGH)
-        gather(1, 3, 4)
-        quantise_x(1, LOW)
+        cast_x(FIRST, HIGH)
+        cast_x(FIRST, LOW)
+        quantise_x(FIRST, HIGH)
+        quantise_x(FIRST, LOW)
+        gather(FIRST, 3, 4)
+        gather(FIRST, 2, 3)
+        gather(FIRST, 0, 2)
+        cast_x(SECOND, HIGH)
+        cast_x(SECOND, LOW)
+        quantise_x(SECOND, HIGH)
+        gather(SECOND, 3, 4)
+        quantise_x(SECOND, LOW)
         for t in (2, 1, 0):
-            gather(1, t, t + 1)
+            gather(SECOND, t, t + 1)
 
         for t in (3, 2, 1, 0):
-            sum_a(t, 0)
-        sum_b(3, 0)
-        finish_tile(3, (1,))
-        sum_b(2, 0)
-        sum_b(1, 0)
-        finish_tile(2, (1,))
-        finish_tile(1, (1,))
-        finish_tile(0, (0, 1))
+            sum_a(t, FIRST)
+        sum_b(3, FIRST)
+        finish_tile(3, (SECOND,))
+        sum_b(2, FIRST)
+        sum_b(1, FIRST)
+        finish_tile(2, (SECOND,))
+        finish_tile(1, (SECOND,))
+        finish_tile(0, (FIRST, SECOND))
 
         for first_tile, end_tile in ((2, 4), (1, 2), (0, 1)):
             turn(first_tile, end_tile)

@@ -28,7 +28,7 @@ OFFSETS_A_COLUMN = 16
 FLOPS = 2 * T * (2 * K * H + H * N)
 BYTES = 4 * K * T + 2 * E * (K * H // 2 + K * H // 32) + E * (H * N // 2 + H * N // 32) + 4 * P * T + 2 * P * (T // 16) + 4 * N * T
 
-VECTOR_TOKENS = {FIRST: (64, 256), SECOND: (48, 160)}
+VECTOR_TOKENS = {FIRST: (64, 256), SECOND: (32, 96)}
 
 
 def tile_moe_rag_glu_silu_kernel(

@@ -119,8 +119,8 @@ def tile_moe_rag_glu_silu_kernel(
             for copy, lo, hi in ((nc.scalar.copy, share, HALF), (nc.vector.tensor_copy, 0, share)):
                 if hi > lo:
                     copy(
-                        x_grouped[s, half][:, lo:hi, :].rearrange("p (c i) j -> p c j i", i=4),
-                        x_raw[s][:, :, half * HALF + lo : half * HALF + hi].rearrange("p j (c i) -> p c j i", i=4),
+                        x_grouped[s, half][:, lo:hi, :].rearrange("p (c i) j -> p c j i", i=2),
+                        x_raw[s][:, :, half * HALF + lo : half * HALF + hi].rearrange("p j (c i) -> p c j i", i=2),
                     )
 
         def quantise_x(s, half):
@@ -162,13 +162,17 @@ def tile_moe_rag_glu_silu_kernel(
 
         def silu(t):
             silu_a[t] = keep.tile([P, H], F32, name=f"silu_a_{t}")
-            nc.scalar.activation(silu_a[t][:], bank_a[t][:], ACT.Silu)
+            nc.scalar.activation(
+                silu_a[t][:].rearrange("p (u q d) -> p u q d", u=2, d=2),
+                bank_a[t][:].rearrange("p (q u d) -> p u q d", u=2, d=2),
+                ACT.Silu,
+            )
 
         def multiply(t):
             hidden[t] = keep.tile([P, 2, P, 2], BF16, name=f"h_{t}", align_bytes=64)
             nc.vector.tensor_tensor(
                 hidden[t][:],
-                silu_a[t][:].rearrange("p (q u d) -> p u q d", u=2, d=2),
+                silu_a[t][:].rearrange("p (u q d) -> p u q d", u=2, d=2),
                 bank_b[t][:].rearrange("p (q u d) -> p u q d", u=2, d=2),
                 MULT,
             )

@@ -21,6 +21,7 @@ PASSES = K // 512
 HALF = T // 2
 LOW, HIGH = 0, 1
 FIRST, SECOND = 1, 0
+EARLY_PLANE = E * PASSES - 1
 TILES = T // P
 BLOCKS = N // P
 OFFSETS_A_COLUMN = 16
@@ -28,7 +29,7 @@ OFFSETS_A_COLUMN = 16
 FLOPS = 2 * T * (2 * K * H + H * N)
 BYTES = 4 * K * T + 2 * E * (K * H // 2 + K * H // 32) + E * (H * N // 2 + H * N // 32) + 4 * P * T + 2 * P * (T // 16) + 4 * N * T
 
-VECTOR_TOKENS = {FIRST: (64, 256), SECOND: (32, 96)}
+VECTOR_TOKENS = {FIRST: (80, 256), SECOND: (64, 48)}
 
 
 def tile_moe_rag_glu_silu_kernel(
@@ -61,11 +62,11 @@ def tile_moe_rag_glu_silu_kernel(
             for s in range(first_pass, end_pass):
                 held[e, s] = codes[:, s - first_pass, :]
 
-        w1_early = scale_tile("w1", w1_scales, 3, 4)
-        w1_rest = scale_tile("w1", w1_scales, 0, 3)
-        w3_all = scale_tile("w3", w3_scales, 0, 4)
-        w2_sc = scale_tile("w2", w2_scales, 0, 2)
-        w1_sc = [w1_rest[:, 0, :], w1_rest[:, 1, :], w1_rest[:, 2, :], w1_early[:, 0, :]]
+        w1_early = scale_tile("w1", w1_scales, EARLY_PLANE, EARLY_PLANE + 1)
+        w3_all = scale_tile("w3", w3_scales, 0, E * PASSES)
+        w1_rest = scale_tile("w1", w1_scales, 0, EARLY_PLANE)
+        w2_sc = scale_tile("w2", w2_scales, 0, E)
+        w1_sc = [w1_rest[:, plane, :] for plane in range(EARLY_PLANE)] + [w1_early[:, 0, :]]
         w3_sc = [w3_all[:, plane, :] for plane in range(E * PASSES)]
         all_words, all_bytes, slot_words, slot_bytes = [], [], {}, {}
         for s in range(PASSES):
@@ -78,18 +79,18 @@ def tile_moe_rag_glu_silu_kernel(
         x_raw, w1, w3 = {}, {}, {}
         x_raw[FIRST] = load_x(FIRST)
         nc.sync.dma_start(offsets[:], offs)
-        load_scales(w1_early, w1_scales, 3, 4)
-        load_words("w1", w1, w1_words, 1, FIRST, FIRST + 1)
+        load_scales(w1_early, w1_scales, EARLY_PLANE, EARLY_PLANE + 1)
         x_raw[SECOND] = load_x(SECOND)
-        load_scales(w1_rest, w1_scales, 0, 3)
-        load_words("w1", w1, w1_words, 0, FIRST, FIRST + 1)
-        load_scales(w3_all, w3_scales, 0, 4)
+        load_words("w1", w1, w1_words, 1, FIRST, FIRST + 1)
         load_words("w3", w3, w3_words, 1, FIRST, FIRST + 1)
+        load_words("w1", w1, w1_words, 0, FIRST, FIRST + 1)
+        load_scales(w3_all, w3_scales, 0, E * PASSES)
         load_words("w1", w1, w1_words, 1, SECOND, SECOND + 1)
+        load_scales(w1_rest, w1_scales, 0, EARLY_PLANE)
         load_words("w3", w3, w3_words, 1, SECOND, SECOND + 1)
         load_words("w1", w1, w1_words, 0, SECOND, SECOND + 1)
-        load_words("w3", w3, w3_words, 0, 0, 2)
-        load_scales(w2_sc, w2_scales, 0, 2)
+        load_words("w3", w3, w3_words, 0, 0, PASSES)
+        load_scales(w2_sc, w2_scales, 0, E)
         w2 = keep.tile([P, E, 2 * N], U8, name="w2", align_bytes=64)
         nc.sync.dma_start(w2[:].bitcast(I32), w2_words.bitcast(I32)[:, 0].rearrange("e p b -> p e b"))
         gate_sb = keep.tile([P, T], F32, name="gate_sb")
@@ -256,12 +257,11 @@ def tile_moe_rag_glu_silu_kernel(
         for t in (2, 1, 0):
             gather(SECOND, t, t + 1)
 
-        for t in (3, 2, 1, 0):
+        for t in (3, 2, 1):
             sum_a(t, FIRST)
-        sum_b(3, FIRST)
+            sum_b(t, FIRST)
         finish_tile(3, (SECOND,))
-        sum_b(2, FIRST)
-        sum_b(1, FIRST)
+        sum_a(0, FIRST)
         finish_tile(2, (SECOND,))
         finish_tile(1, (SECOND,))
         finish_tile(0, (FIRST, SECOND))

from contextlib import ExitStack

import concourse.mybir as mybir
from concourse.masks import make_identity

K, T, E, H, N = 1024, 512, 2, 512, 384

F32 = mybir.dt.float32
BF16 = mybir.dt.bfloat16
I32 = mybir.dt.int32
U32 = mybir.dt.uint32
U16 = mybir.dt.uint16
U8 = mybir.dt.uint8
FP8X4 = mybir.dt.float8_e4m3fn_x4
FP4X4 = mybir.dt.float4_e2m1fn_x4
ACT = mybir.ActivationFunctionType
MULT = mybir.AluOpType.mult

P = 128
PASSES = K // 512
HALF = T // 2
LOW, HIGH = 0, 1
FIRST, SECOND = 1, 0
EARLY_PLANE = E * PASSES - 1
TILES = T // P
BLOCKS = N // P
OFFSETS_A_COLUMN = 16

FLOPS = 2 * T * (2 * K * H + H * N)
BYTES = 4 * K * T + 2 * E * (K * H // 2 + K * H // 32) + E * (H * N // 2 + H * N // 32) + 4 * P * T + 2 * P * (T // 16) + 4 * N * T

VECTOR_TOKENS = {FIRST: (80, 256), SECOND: (64, 48)}


def tile_moe_rag_glu_silu_kernel(
    tc, xT, w1_words, w1_scales, w3_words, w3_scales, w2_words, w2_scales, gate, offs, out
):
    nc = tc.nc
    with ExitStack() as ctx:
        keep = ctx.enter_context(tc.tile_pool(name="keep", bufs=1))
        psum = ctx.enter_context(tc.psum_pool(name="psum", bufs=1))

        def scale_tile(name, scales, first, end):
            tile = keep.tile([P, end - first, scales.shape[3]], U8, name=f"{name}_scales_{first}", align_bytes=64)
            nc.vector.memset(tile[:].bitcast(I32), 0)
            return tile

        def load_scales(tile, scales, first, end):
            rows = scales.bitcast(I32).rearrange("e s (g r) i -> r g (e s) i", r=4)
            for r in range(4):
                nc.sync.dma_start(tile[r:P:32, :, :].bitcast(I32), rows[r][:, first:end, :])

        def load_x(s):
            rows = xT[s * 512 : (s + 1) * 512, :].rearrange("(p j) w -> p j w", j=4)
            raw = keep.tile([P, 4, T], F32, name=f"x_raw_{s}")
            nc.sync.dma_start(raw[:], rows)
            return raw

        def load_words(name, held, words, e, first_pass, end_pass):
            codes = keep.tile([P, end_pass - first_pass, words.shape[3]], U8, name=f"{name}_codes_{e}_{first_pass}", align_bytes=64)
            nc.sync.dma_start(codes[:].bitcast(I32), words.bitcast(I32)[e, first_pass:end_pass].rearrange("s p b -> p s b"))
            for s in range(first_pass, end_pass):
                held[e, s] = codes[:, s - first_pass, :]

        w1_early = scale_tile("w1", w1_scales, EARLY_PLANE, EARLY_PLANE + 1)
        w3_all = scale_tile("w3", w3_scales, 0, E * PASSES)
        w1_rest = scale_tile("w1", w1_scales, 0, EARLY_PLANE)
        w2_sc = scale_tile("w2", w2_scales, 0, E)
        w1_sc = [w1_rest[:, plane, :] for plane in range(EARLY_PLANE)] + [w1_early[:, 0, :]]
        w3_sc = [w3_all[:, plane, :] for plane in range(E * PASSES)]
        all_words, all_bytes, slot_words, slot_bytes = [], [], {}, {}
        for s in range(PASSES):
            all_words.append(keep.tile([P, T], I32, name=f"all_words_{s}", align_bytes=64))
            all_bytes.append(keep.tile([P, T], U8, name=f"all_bytes_{s}", align_bytes=64))
            nc.vector.memset(all_bytes[s][:].bitcast(I32), 0)
        nc.vector.memset(all_words[SECOND][:, 0:HALF], 0)

        offsets = keep.tile([P, T // OFFSETS_A_COLUMN], U16, name="offsets")
        x_raw, w1, w3 = {}, {}, {}
        x_raw[FIRST] = load_x(FIRST)
        nc.sync.dma_start(offsets[:], offs)
        load_scales(w1_early, w1_scales, EARLY_PLANE, EARLY_PLANE + 1)
        x_raw[SECOND] = load_x(SECOND)
        load_words("w1", w1, w1_words, 1, FIRST, FIRST + 1)
        load_words("w3", w3, w3_words, 1, FIRST, FIRST + 1)
        load_words("w1", w1, w1_words, 0, FIRST, FIRST + 1)
        load_scales(w3_all, w3_scales, 0, E * PASSES)
        load_words("w1", w1, w1_words, 1, SECOND, SECOND + 1)
        load_scales(w1_rest, w1_scales, 0, EARLY_PLANE)
        load_words("w3", w3, w3_words, 1, SECOND, SECOND + 1)
        load_words("w1", w1, w1_words, 0, SECOND, SECOND + 1)
        load_words("w3", w3, w3_words, 0, 0, PASSES)
        load_scales(w2_sc, w2_scales, 0, E)
        w2 = keep.tile([P, E, 2 * N], U8, name="w2", align_bytes=64)
        nc.sync.dma_start(w2[:].bitcast(I32), w2_words.bitcast(I32)[:, 0].rearrange("e p b -> p e b"))
        gate_sb = keep.tile([P, T], F32, name="gate_sb")
        nc.sync.dma_start(gate_sb[:], gate[0:P, :])

        ident = keep.tile([P, P], F32, name="ident")
        make_identity(nc, ident[:])

        out_sb = [keep.tile([P, T], F32, name=f"out_sb_{n}") for n in range(BLOCKS)]
        low_sb = [keep.tile([P, HALF], F32, name=f"low_sb_{n}") for n in range(BLOCKS)]
        nc.vector.memset(out_sb[0][:, 0:HALF], 0.0)
        for n in range(1, BLOCKS):
            nc.scalar.activation(out_sb[n][:, 0:HALF], out_sb[0][:, 0:HALF], ACT.Silu)
        bank_a = [psum.tile([P, H], F32, name=f"bank_a_{t}") for t in range(TILES)]
        bank_b = [psum.tile([P, H], F32, name=f"bank_b_{t}") for t in range(TILES)]
        x_grouped, silu_a, hidden, h_grouped, h_codes, y_sb = {}, {}, {}, {}, {}, {}

        def expert_of(t):
            return 0 if t == 0 else 1

        def offsets_of(first_tile, end_tile):
            return offsets[:, first_tile * P // OFFSETS_A_COLUMN : end_tile * P // OFFSETS_A_COLUMN]

        def cast_x(s, half):
            x_grouped[s, half] = keep.tile([P, HALF, 4], BF16, name=f"x_grouped_{s}_{half}", align_bytes=64)
            share = VECTOR_TOKENS[s][half]
            for copy, lo, hi in ((nc.scalar.copy, share, HALF), (nc.vector.tensor_copy, 0, share)):
                if hi > lo:
                    copy(
                        x_grouped[s, half][:, lo:hi, :].rearrange("p (c i) j -> p c j i", i=2),
                        x_raw[s][:, :, half * HALF + lo : half * HALF + hi].rearrange("p j (c i) -> p c j i", i=2),
                    )

        def quantise_x(s, half):
            cols = slice(half * HALF, (half + 1) * HALF)
            nc.vector.quantize_mx(
                out=all_words[s][:, cols].bitcast(FP8X4),
                scales=all_bytes[s][:, cols],
                in_=x_grouped[s, half][:].rearrange("p w j -> p (w j)"),
            )

        def gather(s, first_tile, end_tile):
            slots = (end_tile - first_tile) * P
            words = keep.tile([P, slots], U32, name=f"slot_words_{s}_{first_tile}", align_bytes=64)
            nc.vector.tensor_copy(words[:], all_words[s][:].bitcast(U32).indirect(offsets_of(first_tile, end_tile)))
            scale_bytes = keep.tile([P, slots], U8, name=f"slot_bytes_{s}_{first_tile}", align_bytes=64)
            nc.vector.tensor_copy(scale_bytes[:], all_bytes[s][:].indirect(offsets_of(first_tile, end_tile)))
            for t in range(first_tile, end_tile):
                cols = slice((t - first_tile) * P, (t - first_tile + 1) * P)
                slot_words[s, t] = words[:, cols]
                slot_bytes[s, t] = scale_bytes[:, cols]

        def first_layer(t, s, bank, codes, scales):
            e = expert_of(t)
            nc.tensor.matmul_mx(
                out=bank[t][:],
                lhsT=slot_words[s, t].bitcast(FP8X4),
                lhsT_scale=slot_bytes[s, t],
                rhs=codes[e, s].bitcast(FP4X4),
                rhs_scale=scales[PASSES * e + s],
                start=(s == FIRST),
                stop=(s == SECOND),
            )

        def sum_a(t, s):
            first_layer(t, s, bank_a, w1, w1_sc)

        def sum_b(t, s):
            first_layer(t, s, bank_b, w3, w3_sc)

        def silu(t):
            silu_a[t] = keep.tile([P, H], F32, name=f"silu_a_{t}")
            nc.scalar.activation(
                silu_a[t][:].rearrange("p (u q d) -> p u q d", u=2, d=2),
                bank_a[t][:].rearrange("p (q u d) -> p u q d", u=2, d=2),
                ACT.Silu,
            )

        def multiply(t):
            hidden[t] = keep.tile([P, 2, P, 2], BF16, name=f"h_{t}", align_bytes=64)
            nc.vector.tensor_tensor(
                hidden[t][:],
                silu_a[t][:].rearrange("p (u q d) -> p u q d", u=2, d=2),
                bank_b[t][:].rearrange("p (q u d) -> p u q d", u=2, d=2),
                MULT,
            )

        def finish_tile(t, b_passes):
            sum_a(t, SECOND)
            silu(t)
            for s in b_passes:
                sum_b(t, s)
            multiply(t)

        def turn(first_tile, end_tile):
            h_grouped[first_tile] = keep.tile([P, (end_tile - first_tile) * P, 4], BF16, name=f"h_grouped_{first_tile}", align_bytes=64)
            for t in reversed(range(first_tile, end_tile)):
                pairs = hidden[t][:].rearrange("p u q d -> p (u q d)").bitcast(F32)
                for u in range(2):
                    nc.tensor.transpose(bank_a[t][:, u * P : (u + 1) * P], pairs[:, u * P : (u + 1) * P], ident[:])
                nc.scalar.copy(
                    h_grouped[first_tile][:, (t - first_tile) * P : (t - first_tile + 1) * P, :].bitcast(F32),
                    bank_a[t][:, 0 : 2 * P].rearrange("p (u r) -> p r u", u=2),
                )

        def quantise_h(first_tile, end_tile):
            slots = (end_tile - first_tile) * P
            h_words = keep.tile([P, slots], U32, name=f"h_words_{first_tile}", align_bytes=64)
            h_bytes = keep.tile([P, slots], U8, name=f"h_bytes_{first_tile}", align_bytes=64)
            nc.vector.quantize_mx(
                out=h_words[:].bitcast(FP8X4), scales=h_bytes[:], in_=h_grouped[first_tile][:].rearrange("p r j -> p (r j)")
            )
            h_codes[first_tile] = (h_words, h_bytes)

        def second_layer(first_tile, sums):
            e = expert_of(first_tile)
            h_words, h_bytes = h_codes[first_tile]
            for n in range(BLOCKS):
                nc.tensor.matmul_mx(
                    out=sums[n],
                    lhsT=w2[:, e, 2 * P * n : 2 * P * (n + 1)].bitcast(FP4X4),
                    lhsT_scale=w2_sc[:, e, P * n : P * (n + 1)],
                    rhs=h_words[:].bitcast(FP8X4),
                    rhs_scale=h_bytes[:],
                    start=True,
                    stop=True,
                )

        def second_layer_of_tiles_2_and_3():
            sums = [bank[:, 0 : 2 * P] for bank in (bank_b[3], bank_b[2], bank_a[3])]
            second_layer(2, sums)
            for n in range(BLOCKS):
                y = keep.tile([P, 2 * P], F32, name=f"y_2_{n}")
                nc.scalar.copy(y[:], sums[n])
                y_sb[2, n] = y[:]

        def second_layer_of_tile(t, bank):
            second_layer(t, [bank[:, n * P : (n + 1) * P] for n in range(BLOCKS)])
            y = keep.tile([P, N], F32, name=f"y_{t}")
            nc.scalar.copy(y[:], bank[:, 0:N])
            for n in range(BLOCKS):
                y_sb[t, n] = y[:, n * P : (n + 1) * P]

        def scatter(window, first_tile, end_tile, n):
            nc.vector.tensor_tensor(
                window[:].indirect(offsets_of(first_tile, end_tile)),
                y_sb[first_tile, n],
                gate_sb[:, first_tile * P : end_tile * P],
                MULT,
            )

        cast_x(FIRST, HIGH)
        cast_x(FIRST, LOW)
        quantise_x(FIRST, HIGH)
        quantise_x(FIRST, LOW)
        gather(FIRST, 3, 4)
        gather(FIRST, 2, 3)
        gather(FIRST, 0, 2)
        cast_x(SECOND, HIGH)
        cast_x(SECOND, LOW)
        quantise_x(SECOND, HIGH)
        gather(SECOND, 3, 4)
        quantise_x(SECOND, LOW)
        for t in (2, 1, 0):
            gather(SECOND, t, t + 1)

        for t in (3, 2, 1):
            sum_a(t, FIRST)
            sum_b(t, FIRST)
        finish_tile(3, (SECOND,))
        sum_a(0, FIRST)
        finish_tile(2, (SECOND,))
        finish_tile(1, (SECOND,))
        finish_tile(0, (FIRST, SECOND))

        for first_tile, end_tile in ((2, 4), (1, 2), (0, 1)):
            turn(first_tile, end_tile)
            quantise_h(first_tile, end_tile)
        second_layer_of_tiles_2_and_3()
        second_layer_of_tile(0, bank_b[0])
        second_layer_of_tile(1, bank_b[2])

        for first_tile, end_tile in ((2, 4), (0, 1)):
            for n in range(BLOCKS):
                scatter(out_sb[n], first_tile, end_tile, n)
        for n in range(BLOCKS):
            nc.sync.dma_start(out[n * P : (n + 1) * P, HALF:T], out_sb[n][:, HALF:T])
            nc.scalar.copy(low_sb[n][:], out_sb[n][:, 0:HALF])
        for n in range(BLOCKS):
            scatter(low_sb[n], 1, 2, n)
            nc.sync.dma_start(out[n * P : (n + 1) * P, 0:HALF], low_sb[n][:])
